import numpy as np
import ml_dtypes


def mxq(x, axis, fmt="e4m3"):
    dtype, down = {"e4m3": (ml_dtypes.float8_e4m3fn, 7), "e5m2": (ml_dtypes.float8_e5m2, 14)}[fmt]
    v = np.moveaxis(np.asarray(x, np.float32).astype(ml_dtypes.bfloat16).astype(np.float64), axis, -1)
    blocks = v.reshape(v.shape[:-1] + (-1, 32))
    amax = np.abs(blocks).max(-1, keepdims=True)
    byte = np.maximum(np.where(amax > 0, np.frexp(amax)[1] - 1 + 127, 0) - down, 1)
    scale = np.exp2(byte - 127.0)
    codes = (blocks / scale).astype(np.float32).astype(dtype).astype(np.float64)
    return np.moveaxis((codes * scale).reshape(v.shape), -1, axis)


WIDE = False


def mx_kscale(k):
    if not WIDE:
        return np.ones(k)
    levels = np.array([10, -10, 5, -5, 0])
    if k % 512:
        return np.exp2(np.random.permutation(np.resize(levels, k // 32))).repeat(32)
    a = np.empty((k // 512, 16))
    for p in range(k // 512):
        a[p, :8] = np.random.permutation(np.resize(levels, 8))
        for g in range(8):
            far = levels[np.abs(levels - a[p, g]) >= 10]
            a[p, g + 8] = far[np.random.randint(len(far))]
    return np.exp2(a.ravel()).repeat(32)


def f64(x):
    return np.asarray(x).astype(np.float64)


def striped(idx):
    return np.tile(idx.reshape(-1, 16).T, (8, 1)).astype(np.uint16)


def unstriped(offs):
    return offs[:16].T.reshape(-1).astype(np.int64)


E2M1 = np.array([0.0, 0.5, 1.0, 1.5, 2.0, 3.0, 4.0, 6.0, -0.0, -0.5, -1.0, -1.5, -2.0, -3.0, -4.0, -6.0])


def pack_weight(w, fmt):
    k, n = w.shape
    w = f64(np.asarray(w, np.float32).astype(ml_dtypes.bfloat16)).reshape(k // 32, 32, n)
    amax = np.abs(w).max(1)
    if fmt == "e4m3":
        byte = np.frexp(amax)[1] - 1 + 127 - 7
    else:
        mant, ex = np.frexp(amax / 6.0)
        byte = np.where(mant > 0.5, ex, ex - 1) + 127
    byte = np.clip(np.where(amax > 0, byte, 1), 1, 254)
    scaled = (w * np.exp2(127.0 - byte)[:, None, :]).reshape(k, n).astype(np.float32)
    by_word = np.ascontiguousarray(scaled.reshape(k // 512, 128, 4, n).transpose(0, 1, 3, 2))
    if fmt == "e4m3":
        words = by_word.astype(ml_dtypes.float8_e4m3fn).view(np.uint8)
    else:
        c = by_word.astype(ml_dtypes.float4_e2m1fn).view(np.uint8) & 0xF
        words = (c[..., 0::2] | (c[..., 1::2] << 4)).reshape(k // 512, 128, 2 * n)
    return np.ascontiguousarray(words), np.ascontiguousarray(byte.astype(np.uint8).reshape(k // 512, 16, n))


def unpack_weight(words, scales, fmt):
    g, _, n = scales.shape
    words = np.ascontiguousarray(words).reshape(g, 128, n, -1)
    if fmt == "e4m3":
        vals = words.view(ml_dtypes.float8_e4m3fn).astype(np.float64)
    else:
        nib = np.empty((g, 128, n, 4), np.uint8)
        nib[..., 0::2] = words & 0xF
        nib[..., 1::2] = words >> 4
        vals = E2M1[nib]
    vals = vals * np.repeat(np.exp2(scales.astype(np.float64) - 127.0), 8, axis=1)[..., None]
    return vals.transpose(0, 1, 3, 2).reshape(g * 512, n)


def gelu(v):
    return 0.5 * v * (1.0 + np.tanh(np.sqrt(2.0 / np.pi) * (v + 0.044715 * v**3)))


K, K2, H, N, T, T2, S, P = 1024, 512, 1024, 512, 2048, 1024, 512, 512

def setup_inputs():
    n = np.random.standard_normal
    s = mx_kscale(K)[:, None]
    s2 = mx_kscale(K2)[:, None]
    u = mx_kscale(H)[:, None]
    tab_words, tab_scales = pack_weight(n((K, T)) * s, "e4m3")
    w2_words, w2_scales = pack_weight(n((K, H)) / np.sqrt(K) / s * u.T, "e2m1")
    wo_words, wo_scales = pack_weight(1.5 * n((H, N)) / np.sqrt(H) / u, "e4m3")
    return {
        "tab_words": tab_words, "tab_scales": tab_scales,
        "offs": striped(np.random.permutation(T)[:P]),
        "offs2": striped(np.random.permutation(T2)[:S]),
        "offs3": striped(np.random.permutation(T2)[:P]),
        "xs": (np.round(16 * n((K2, S))) / 16 * s2).astype(np.float32),
        "base": (n((K2, T2)) * s2).astype(np.float32),
        "w1": (n((K2, H)) / np.sqrt(K2) / s2 * u.T).astype(np.float32),
        "w2_words": w2_words, "w2_scales": w2_scales,
        "nf": (0.5 * np.exp(0.3 * n(H)) * u[:, 0]).astype(np.float32),
        "wo_words": wo_words, "wo_scales": wo_scales,
    }

def reference(tab_words, tab_scales, offs, offs2, offs3, xs, base, w1, w2_words, w2_scales, nf, wo_words, wo_scales):
    page = f64(base).copy()
    page[:, unstriped(offs2)] = f64(xs)
    a = mxq(f64(w1), 0, "e4m3").T @ mxq(page, 0, "e4m3")
    d = a[:, unstriped(offs3)]
    v = unpack_weight(tab_words, tab_scales, "e4m3")[:, unstriped(offs)]
    b = unpack_weight(w2_words, w2_scales, "e2m1").T @ v
    ratio = np.abs(b) / (np.abs(d) + f64(nf)[:, None])
    z = d * np.minimum(ratio, 1.0)
    wo = unpack_weight(wo_words, wo_scales, "e4m3")
    return wo.T @ mxq(z, 0, "e4m3")

@@ -1,0 +1,258 @@
+from contextlib import ExitStack
+
+import concourse.mybir as mybir
+from concourse.masks import make_identity
+
+F32 = mybir.dt.float32
+BF16 = mybir.dt.bfloat16
+I32 = mybir.dt.int32
+U32 = mybir.dt.uint32
+U16 = mybir.dt.uint16
+U8 = mybir.dt.uint8
+E4M3 = mybir.dt.float8_e4m3fn_x4
+E2M1 = mybir.dt.float4_e2m1fn_x4
+ALU = mybir.AluOpType
+ACT = mybir.ActivationFunctionType
+
+P = 128
+T, T2, S, H, N = 2048, 1024, 512, 1024, 512
+FLOPS = 2684354560
+
+
+def tile_list_chirp_interference_repair_kernel(
+    tc, tab_words, tab_scales, offs, offs2, offs3, xs, base, w1, w2_words, w2_scales, nf, wo_words, wo_scales, out
+):
+    nc = tc.nc
+    with ExitStack() as ctx:
+        keep = ctx.enter_context(tc.tile_pool(name="keep", bufs=1))
+        ring = ctx.enter_context(tc.tile_pool(name="ring", bufs=3))
+        psum = ctx.enter_context(tc.psum_pool(name="psum", bufs=4))
+
+        def kt(name, shape, dtype):
+            return keep.tile(shape, dtype, name=name, align_bytes=64)
+
+        idx = keep.tile([P, S // 16], U16, name="idx")
+        idx2 = keep.tile([P, S // 16], U16, name="idx2")
+        idx3 = keep.tile([P, S // 16], U16, name="idx3")
+        page = [kt("page%d" % i, [P, T2], F32) for i in range(4)]
+        new = [kt("new%d" % i, [P, S], F32) for i in range(4)]
+        w1_raw = [kt("w1_raw%d" % a, [P, 4, 512], F32) for a in range(2)]
+        tabw = [kt("tabw%d" % a, [P, T], I32) for a in range(2)]
+        tabs = kt("tabs", [P, 2, T], U8)
+        w2w = kt("w2w", [P, 2, 2 * H], U8)
+        w2s = kt("w2s", [P, 2, H], U8)
+        wow = kt("wow", [P, 2, N], I32)
+        wos = kt("wos", [P, 2, N], U8)
+        floor = kt("floor", [P, 2, 4], F32)
+        ident = kt("ident", [P, P], F32)
+        warm = kt("warm", [P, 8], F32)
+
+        nc.gpsimd.memset(warm[:], 1.0)
+        nc.scalar.activation(warm[:, 4:5], warm[:, 0:1], ACT.Abs_reciprocal_sqrt)
+        nc.vector.memset(tabs[:].rearrange("p a t -> p (a t)").bitcast(I32), 0)
+        nc.gpsimd.memset(w2s[:].rearrange("p a t -> p (a t)").bitcast(I32), 0)
+        nc.gpsimd.memset(wos[:].rearrange("p a t -> p (a t)").bitcast(I32), 0)
+
+        base_rows = base.rearrange("(p i) t -> p i t", i=4)
+        xs_rows = xs.rearrange("(p i) t -> p i t", i=4)
+        w1_rows = w1.rearrange("(p i) r -> p i r", i=4)
+
+        def load_plane(i):
+            nc.sync.dma_start(new[i][:], xs_rows[:, i, :])
+            nc.sync.dma_start(page[i][:], base_rows[:, i, :])
+
+        def load_scales(tile, dram):
+            for q in range(4):
+                nc.gpsimd.dma_start(
+                    tile[32 * q : 32 * q + 4, :, :].bitcast(I32),
+                    dram[:, 4 * q : 4 * q + 4, :].rearrange("a r c -> r a c").bitcast(I32),
+                )
+
+        def load_tab(a):
+            nc.sync.dma_start(tabw[a][:], tab_words[a].rearrange("p t i -> p (t i)").bitcast(I32))
+
+        nc.sync.dma_start(idx2[:], offs2)
+        load_plane(0)
+        load_plane(1)
+        nc.sync.dma_start(idx[:], offs)
+        nc.sync.dma_start(w1_raw[0][:], w1_rows[:, :, 0:512])
+        load_tab(0)
+        load_tab(1)
+        nc.sync.dma_start(w2w[:].bitcast(I32), w2_words.rearrange("a p c -> p a c").bitcast(I32))
+        load_plane(2)
+        load_plane(3)
+        nc.sync.dma_start(idx3[:], offs3)
+        nc.sync.dma_start(w1_raw[1][:], w1_rows[:, :, 512:1024])
+        nc.sync.dma_start(wow[:], wo_words.rearrange("a p n i -> p a (n i)").bitcast(I32))
+        load_scales(tabs, tab_scales)
+        load_scales(w2s, w2_scales)
+        nc.gpsimd.dma_start(floor[:], nf.rearrange("(a p t) -> p a t", a=2, t=4))
+        load_scales(wos, wo_scales)
+        make_identity(nc, ident[:])
+
+        page_planes = kt("page_planes", [P, 4, T2], BF16)
+
+        def land(i):
+            nc.vector.tensor_copy(page[i][:].indirect(idx2[:]), new[i][:])
+            nc.scalar.copy(page_planes[:, i, :], page[i][:])
+
+        w1_bf = [kt("w1_bf%d" % a, [P, 2048], BF16) for a in range(2)]
+        w1_codes = [kt("w1_codes%d" % a, [P, 512], U32) for a in range(2)]
+        w1_sc = [kt("w1_sc%d" % a, [P, 512], U8) for a in range(2)]
+
+        def round_w1(a):
+            nc.scalar.copy(
+                w1_bf[a][:].rearrange("p (t m j) -> p m j t", t=4, j=4),
+                w1_raw[a][:].rearrange("p j (m t) -> p m j t", t=4),
+            )
+
+        def quant_w1(a):
+            nc.vector.quantize_mx(out=w1_codes[a][:].bitcast(E4M3), scales=w1_sc[a][:], in_=w1_bf[a][:])
+
+        land(0)
+        round_w1(0)
+        land(1)
+
+        vw = [kt("vw%d" % a, [P, S], U32) for a in range(2)]
+        vs = [kt("vs%d" % a, [P, S], U8) for a in range(2)]
+        for a in range(2):
+            nc.vector.tensor_copy(vs[a][:], tabs[:, a, :].indirect(idx[:]))
+        for a in range(2):
+            nc.vector.tensor_copy(vw[a][:], tabw[a][:].bitcast(U32).indirect(idx[:]))
+
+        clean = [kt("clean%d" % jt, [P, 2, 4, P], F32) for jt in range(4)]
+        for h in range(2):
+            for jt in range(4):
+                bank = psum.tile([P, 512], F32, name="bank_b", tag="y")
+                cols = slice(P * jt, P * jt + P)
+                for a in range(2):
+                    nc.tensor.matmul_mx(
+                        out=bank[:],
+                        lhsT=vw[a][:, cols].bitcast(E4M3),
+                        lhsT_scale=vs[a][:, cols],
+                        rhs=w2w[:, a, 1024 * h : 1024 * h + 1024].bitcast(E2M1),
+                        rhs_scale=w2s[:, a, 512 * h : 512 * h + 512],
+                        start=(a == 0),
+                        stop=(a == 1),
+                    )
+                nc.scalar.activation(clean[jt][:, h, :, :], bank[:].rearrange("p (m t) -> p t m", t=4), ACT.Abs)
+
+        land(2)
+        land(3)
+        quant_w1(0)
+
+        page_bf = [kt("page_bf%d" % h, [P, 2048], BF16) for h in range(2)]
+        page_codes = [kt("page_codes%d" % h, [P, 512], U32) for h in range(2)]
+        page_sc = [kt("page_sc%d" % h, [P, 512], U8) for h in range(2)]
+
+        def weave(dst, src):
+            nc.vector.tensor_copy(
+                dst.rearrange("p (c i t) -> p c t i", i=4, t=4), src.rearrange("p t (c i) -> p c t i", i=4)
+            )
+
+        for h in range(2):
+            weave(page_bf[h][:], page_planes[:, :, 512 * h : 512 * h + 512])
+        for h in range(2):
+            nc.vector.quantize_mx(out=page_codes[h][:].bitcast(E4M3), scales=page_sc[h][:], in_=page_bf[h][:])
+        round_w1(1)
+        quant_w1(1)
+
+        dirty = [kt("dirty%d" % k, [P, S], F32) for k in range(8)]
+        z_planes = [kt("z_planes%d" % a, [P, 4, S], BF16) for a in range(2)]
+        z_bf = [kt("z_bf%d" % a, [P, 2048], BF16) for a in range(2)]
+        z_codes = [kt("z_codes%d" % a, [P, S], U32) for a in range(2)]
+        z_sc = [kt("z_sc%d" % a, [P, S], U8) for a in range(2)]
+        recips = {}
+
+        projs, mags, roots = {}, {}, {}
+
+        def project(k, h):
+            a, t = divmod(k, 4)
+            if h == 0:
+                projs[k] = ring.tile([P, T2], F32, name="proj", align_bytes=64)
+            bank = psum.tile([P, 512], F32, name="bank_a", tag="x")
+            nc.tensor.matmul_mx(
+                out=bank[:],
+                lhsT=w1_codes[a][:, P * t : P * t + P].bitcast(E4M3),
+                lhsT_scale=w1_sc[a][:, P * t : P * t + P],
+                rhs=page_codes[h][:].bitcast(E4M3),
+                rhs_scale=page_sc[h][:],
+                start=True,
+                stop=True,
+            )
+            nc.scalar.copy(projs[k][:, 512 * h : 512 * h + 512], bank[:])
+
+        def pick(k):
+            nc.vector.tensor_copy(dirty[k][:], projs[k][:].indirect(idx3[:]))
+
+        def magnitude(k):
+            mags[k] = ring.tile([P, S], F32, name="mag", align_bytes=64)
+            nc.scalar.activation(mags[k][:], dirty[k][:], ACT.Abs)
+
+        def inverse_root(k):
+            a, t = divmod(k, 4)
+            roots[k] = ring.tile([P, S], F32, name="root", align_bytes=64)
+            nc.scalar.activation(roots[k][:], mags[k][:], ACT.Abs_reciprocal_sqrt, bias=floor[:, a, t : t + 1])
+
+        def inverse(k):
+            recips[k] = ring.tile([P, S], F32, name="recip", align_bytes=64)
+            nc.scalar.activation(recips[k][:], roots[k][:], ACT.Square)
+
+        def limit(k):
+            a, t = divmod(k, 4)
+            bank = psum.tile([P, 512], F32, name="bank_t", tag="y")
+            for jt in range(4):
+                nc.tensor.transpose(bank[:, P * jt : P * jt + P], clean[jt][:, a, t, :], ident[:])
+            ratio = ring.tile([P, S], F32, name="ratio", align_bytes=64)
+            nc.vector.tensor_tensor(ratio[:], bank[:], recips[k][:], ALU.mult)
+            return ratio
+
+        def shrink(k, ratio):
+            a, t = divmod(k, 4)
+            nc.vector.scalar_tensor_tensor(z_planes[a][:, t, :], ratio[:], 1.0, dirty[k][:], ALU.min, ALU.mult)
+
+        def quant_z(a):
+            weave(z_bf[a][:], z_planes[a][:])
+            nc.vector.quantize_mx(out=z_codes[a][:].bitcast(E4M3), scales=z_sc[a][:], in_=z_bf[a][:])
+
+        ratios = {}
+        live = range(8)
+        for step in range(8 + 4):
+            if step in live:
+                project(step, 0)
+            if step - 2 in live:
+                inverse_root(step - 2)
+            if step - 3 in live:
+                ratios[step - 3] = limit(step - 3)
+            if step - 1 in live:
+                magnitude(step - 1)
+            if step in live:
+                project(step, 1)
+            if step - 2 in live:
+                inverse(step - 2)
+            if step in live:
+                pick(step)
+            if step - 3 in live:
+                shrink(step - 3, ratios[step - 3])
+            if step - 4 in (3, 7):
+                quant_z((step - 4) // 4)
+
+        banks = [psum.tile([P, 512], F32, name="bank_o", tag="x") for nt in range(4)]
+        for a in range(2):
+            for nt in range(4):
+                nc.tensor.matmul_mx(
+                    out=banks[nt][:],
+                    lhsT=wow[:, a, P * nt : P * nt + P].bitcast(E4M3),
+                    lhsT_scale=wos[:, a, P * nt : P * nt + P],
+                    rhs=z_codes[a][:].bitcast(E4M3),
+                    rhs_scale=z_sc[a][:],
+                    start=(a == 0),
+                    stop=(a == 1),
+                )
+        for nt in range(4):
+            res = kt("res%d" % nt, [P, S], F32)
+            if nt % 2 == 0:
+                nc.scalar.copy(res[:], banks[nt][:])
+            else:
+                nc.vector.tensor_copy(res[:], banks[nt][:])
+            nc.sync.dma_start(out[P * nt : P * nt + P, :], res[:])

@@ -28,8 +28,8 @@ def tile_list_chirp_interference_repair_kernel(
         ring = ctx.enter_context(tc.tile_pool(name="ring", bufs=3))
         psum = ctx.enter_context(tc.psum_pool(name="psum", bufs=4))
 
-        def kt(name, shape, dtype):
-            return keep.tile(shape, dtype, name=name, align_bytes=64)
+        def kt(name, shape, dtype, tag=None):
+            return keep.tile(shape, dtype, name=name, tag=tag or name, align_bytes=64)
 
         idx = keep.tile([P, S // 16], U16, name="idx")
         idx2 = keep.tile([P, S // 16], U16, name="idx2")
@@ -38,7 +38,10 @@ def tile_list_chirp_interference_repair_kernel(
         new = [kt("new%d" % i, [P, S], F32) for i in range(4)]
         w1_raw = [kt("w1_raw%d" % a, [P, 4, 512], F32) for a in range(2)]
         tabw = [kt("tabw%d" % a, [P, T], I32) for a in range(2)]
-        tabs = kt("tabs", [P, 2, T], U8)
+        tabs = kt("tabs", [P, T], U8)
+        picked_rows = kt("picked_rows", [P, S], U8)
+        vw = [kt("vw%d" % a, [P, S], U32) for a in range(2)]
+        vs = kt("vs", [P, 2, S], U8)
         w2w = kt("w2w", [P, 2, 2 * H], U8)
         w2s = kt("w2s", [P, 2, H], U8)
         wow = kt("wow", [P, 2, N], I32)
@@ -49,9 +52,12 @@ def tile_list_chirp_interference_repair_kernel(
 
         nc.gpsimd.memset(warm[:], 1.0)
         nc.scalar.activation(warm[:, 4:5], warm[:, 0:1], ACT.Abs_reciprocal_sqrt)
-        nc.vector.memset(tabs[:].rearrange("p a t -> p (a t)").bitcast(I32), 0)
+        nc.vector.memset(tabs[32:64, :].bitcast(I32), 0)
+        nc.vector.memset(tabs[64:128, :].bitcast(I32), 0)
+        nc.vector.memset(vs[:].rearrange("p a t -> p (a t)").bitcast(I32), 0)
         nc.gpsimd.memset(w2s[:].rearrange("p a t -> p (a t)").bitcast(I32), 0)
         nc.gpsimd.memset(wos[:].rearrange("p a t -> p (a t)").bitcast(I32), 0)
+        make_identity(nc, ident[:])
 
         base_rows = base.rearrange("(p i) t -> p i t", i=4)
         xs_rows = xs.rearrange("(p i) t -> p i t", i=4)
@@ -61,115 +67,134 @@ def tile_list_chirp_interference_repair_kernel(
             nc.sync.dma_start(new[i][:], xs_rows[:, i, :])
             nc.sync.dma_start(page[i][:], base_rows[:, i, :])
 
-        def load_scales(tile, dram):
+        def load_scales(queue, tile, dram):
             for q in range(4):
-                nc.gpsimd.dma_start(
+                queue.dma_start(
                     tile[32 * q : 32 * q + 4, :, :].bitcast(I32),
                     dram[:, 4 * q : 4 * q + 4, :].rearrange("a r c -> r a c").bitcast(I32),
                 )
 
+        def load_tab_scales():
+            load_scales(nc.sync, tabs, tab_scales)
+
         def load_tab(a):
             nc.sync.dma_start(tabw[a][:], tab_words[a].rearrange("p t i -> p (t i)").bitcast(I32))
 
+        def load_w1(a):
+            nc.sync.dma_start(w1_raw[a][:], w1_rows[:, :, 512 * a : 512 * a + 512])
+
+        nc.sync.dma_start(tabs[0:32, :].bitcast(I32), tab_scales.rearrange("a q t -> (a q) t").bitcast(I32))
+        nc.sync.dma_start(idx[:], offs)
         nc.sync.dma_start(idx2[:], offs2)
         load_plane(0)
         load_plane(1)
-        nc.sync.dma_start(idx[:], offs)
-        nc.sync.dma_start(w1_raw[0][:], w1_rows[:, :, 0:512])
         load_tab(0)
         load_tab(1)
-        nc.sync.dma_start(w2w[:].bitcast(I32), w2_words.rearrange("a p c -> p a c").bitcast(I32))
         load_plane(2)
+        nc.sync.dma_start(w2w[:].bitcast(I32), w2_words.rearrange("a p c -> p a c").bitcast(I32))
         load_plane(3)
+        load_w1(0)
+        load_w1(1)
         nc.sync.dma_start(idx3[:], offs3)
-        nc.sync.dma_start(w1_raw[1][:], w1_rows[:, :, 512:1024])
+        nc.sync.dma_start(floor[:], nf.rearrange("(a p t) -> p a t", a=2, t=4))
+        load_scales(nc.gpsimd, w2s, w2_scales)
         nc.sync.dma_start(wow[:], wo_words.rearrange("a p n i -> p a (n i)").bitcast(I32))
-        load_scales(tabs, tab_scales)
-        load_scales(w2s, w2_scales)
-        nc.gpsimd.dma_start(floor[:], nf.rearrange("(a p t) -> p a t", a=2, t=4))
-        load_scales(wos, wo_scales)
-        make_identity(nc, ident[:])
+        load_scales(nc.sync, wos, wo_scales)
 
         page_planes = kt("page_planes", [P, 4, T2], BF16)
 
         def land(i):
             nc.vector.tensor_copy(page[i][:].indirect(idx2[:]), new[i][:])
-            nc.scalar.copy(page_planes[:, i, :], page[i][:])
+            if i < 3:
+                nc.gpsimd.tensor_scalar(page_planes[:, i, :], page[i][:], 1.0, 0.0, ALU.mult, ALU.add)
+            else:
+                for h in range(2):
+                    nc.vector.tensor_copy(page_planes[:, i, 512 * h : 512 * h + 512], page[i][:, 512 * h : 512 * h + 512])
 
         w1_bf = [kt("w1_bf%d" % a, [P, 2048], BF16) for a in range(2)]
-        w1_codes = [kt("w1_codes%d" % a, [P, 512], U32) for a in range(2)]
+        w1_codes = {}
         w1_sc = [kt("w1_sc%d" % a, [P, 512], U8) for a in range(2)]
 
         def round_w1(a):
-            nc.scalar.copy(
-                w1_bf[a][:].rearrange("p (t m j) -> p m j t", t=4, j=4),
-                w1_raw[a][:].rearrange("p j (m t) -> p m j t", t=4),
-            )
+            dst = w1_bf[a][:].rearrange("p (t m j) -> p m j t", t=4, j=4)
+            src = w1_raw[a][:].rearrange("p j (m t) -> p m j t", t=4)
+            for m0 in range(0, P, 64):
+                nc.scalar.copy(dst[:, m0 : m0 + 64], src[:, m0 : m0 + 64])
 
         def quant_w1(a):
+            w1_codes[a] = kt("w1_codes%d" % a, [P, 512], U32, tag="new%d" % (a + 2))
             nc.vector.quantize_mx(out=w1_codes[a][:].bitcast(E4M3), scales=w1_sc[a][:], in_=w1_bf[a][:])
 
-        land(0)
-        round_w1(0)
-        land(1)
-
-        vw = [kt("vw%d" % a, [P, S], U32) for a in range(2)]
-        vs = [kt("vs%d" % a, [P, S], U8) for a in range(2)]
-        for a in range(2):
-            nc.vector.tensor_copy(vs[a][:], tabs[:, a, :].indirect(idx[:]))
-        for a in range(2):
-            nc.vector.tensor_copy(vw[a][:], tabw[a][:].bitcast(U32).indirect(idx[:]))
-
         clean = [kt("clean%d" % jt, [P, 2, 4, P], F32) for jt in range(4)]
-        for h in range(2):
-            for jt in range(4):
-                bank = psum.tile([P, 512], F32, name="bank_b", tag="y")
-                cols = slice(P * jt, P * jt + P)
-                for a in range(2):
-                    nc.tensor.matmul_mx(
-                        out=bank[:],
-                        lhsT=vw[a][:, cols].bitcast(E4M3),
-                        lhsT_scale=vs[a][:, cols],
-                        rhs=w2w[:, a, 1024 * h : 1024 * h + 1024].bitcast(E2M1),
-                        rhs_scale=w2s[:, a, 512 * h : 512 * h + 512],
-                        start=(a == 0),
-                        stop=(a == 1),
-                    )
-                nc.scalar.activation(clean[jt][:, h, :, :], bank[:].rearrange("p (m t) -> p t m", t=4), ACT.Abs)
 
-        land(2)
-        land(3)
-        quant_w1(0)
+        def clean_path():
+            for a in range(2):
+                nc.vector.tensor_copy(vw[a][:], tabw[a][:].bitcast(U32).indirect(idx[:]))
+            for h in range(2):
+                for jt in range(4):
+                    bank = psum.tile([P, 512], F32, name="bank_b", tag="y")
+                    cols = slice(P * jt, P * jt + P)
+                    for a in range(2):
+                        nc.tensor.matmul_mx(
+                            out=bank[:],
+                            lhsT=vw[a][:, cols].bitcast(E4M3),
+                            lhsT_scale=vs[:, a, cols],
+                            rhs=w2w[:, a, 1024 * h : 1024 * h + 1024].bitcast(E2M1),
+                            rhs_scale=w2s[:, a, 512 * h : 512 * h + 512],
+                            start=(a == 0),
+                            stop=(a == 1),
+                        )
+                    nc.scalar.activation(clean[jt][:, h, :, :], bank[:].rearrange("p (m t) -> p t m", t=4), ACT.Abs)
 
-        page_bf = [kt("page_bf%d" % h, [P, 2048], BF16) for h in range(2)]
+        page_bf = [kt("page_bf%d" % h, [P, 512, 4], BF16) for h in range(2)]
         page_codes = [kt("page_codes%d" % h, [P, 512], U32) for h in range(2)]
         page_sc = [kt("page_sc%d" % h, [P, 512], U8) for h in range(2)]
 
-        def weave(dst, src):
-            nc.vector.tensor_copy(
-                dst.rearrange("p (c i t) -> p c t i", i=4, t=4), src.rearrange("p t (c i) -> p c t i", i=4)
-            )
+        def weave(dst, src, split):
+            width = dst.shape[1]
+            for copy, c0, c1 in ((nc.vector.tensor_copy, 0, split), (nc.scalar.copy, split, width)):
+                if c0 < c1:
+                    copy(
+                        dst[:, c0:c1, :].rearrange("p (c i) t -> p c t i", i=4),
+                        src[:, :, c0:c1].rearrange("p t (c i) -> p c t i", i=4),
+                    )
 
-        for h in range(2):
-            weave(page_bf[h][:], page_planes[:, :, 512 * h : 512 * h + 512])
-        for h in range(2):
-            nc.vector.quantize_mx(out=page_codes[h][:].bitcast(E4M3), scales=page_sc[h][:], in_=page_bf[h][:])
+        def quant(codes, scales, woven):
+            nc.vector.quantize_mx(out=codes.bitcast(E4M3), scales=scales, in_=woven.rearrange("p c t -> p (c t)"))
+
+        def quant_page():
+            for h in range(2):
+                weave(page_bf[h][:], page_planes[:, :, 512 * h : 512 * h + 512], 512)
+            for h in range(2):
+                quant(page_codes[h][:], page_sc[h][:], page_bf[h][:])
+
+        nc.vector.tensor_copy(picked_rows[:], tabs[:].indirect(idx[:]))
+        for a in range(2):
+            for q in range(4):
+                row = 16 * a + 4 * q
+                nc.scalar.dma_start(vs[32 * q : 32 * q + 4, a, :].bitcast(I32), picked_rows[row : row + 4, :].bitcast(I32))
+        land(0)
+        land(1)
+        clean_path()
+        land(2)
+        land(3)
+        round_w1(0)
         round_w1(1)
+        quant_w1(0)
+        quant_page()
         quant_w1(1)
 
-        dirty = [kt("dirty%d" % k, [P, S], F32) for k in range(8)]
+        dirty = [kt("dirty%d" % u, [P, 2, S], F32) for u in range(4)]
         z_planes = [kt("z_planes%d" % a, [P, 4, S], BF16) for a in range(2)]
-        z_bf = [kt("z_bf%d" % a, [P, 2048], BF16) for a in range(2)]
-        z_codes = [kt("z_codes%d" % a, [P, S], U32) for a in range(2)]
-        z_sc = [kt("z_sc%d" % a, [P, S], U8) for a in range(2)]
-        recips = {}
+        projs = [kt("proj%d" % k, [P, T2], F32) for k in range(8)]
+        mags, roots, recips, ratios = {}, {}, {}, {}
+        last = 7
 
-        projs, mags, roots = {}, {}, {}
+        def spans(k):
+            return [slice(0, 256), slice(256, 512)] if k == last else [slice(0, 512)]
 
         def project(k, h):
             a, t = divmod(k, 4)
-            if h == 0:
-                projs[k] = ring.tile([P, T2], F32, name="proj", align_bytes=64)
             bank = psum.tile([P, 512], F32, name="bank_a", tag="x")
             nc.tensor.matmul_mx(
                 out=bank[:],
@@ -180,79 +205,111 @@ def tile_list_chirp_interference_repair_kernel(
                 start=True,
                 stop=True,
             )
-            nc.scalar.copy(projs[k][:, 512 * h : 512 * h + 512], bank[:])
+            copy = nc.vector.tensor_copy if (h == 1 and k < 2) else nc.scalar.copy
+            copy(projs[k][:, 512 * h : 512 * h + 512], bank[:])
 
         def pick(k):
-            nc.vector.tensor_copy(dirty[k][:], projs[k][:].indirect(idx3[:]))
+            for cols in spans(k):
+                entries = idx3[:, cols.start // 16 : cols.stop // 16]
+                nc.vector.tensor_copy(dirty[k // 2][:, k % 2, cols], projs[k][:].indirect(entries))
 
         def magnitude(k):
             mags[k] = ring.tile([P, S], F32, name="mag", align_bytes=64)
-            nc.scalar.activation(mags[k][:], dirty[k][:], ACT.Abs)
+            for cols in spans(k):
+                nc.scalar.activation(mags[k][:, cols], dirty[k // 2][:, k % 2, cols], ACT.Abs)
 
         def inverse_root(k):
             a, t = divmod(k, 4)
             roots[k] = ring.tile([P, S], F32, name="root", align_bytes=64)
-            nc.scalar.activation(roots[k][:], mags[k][:], ACT.Abs_reciprocal_sqrt, bias=floor[:, a, t : t + 1])
+            for cols in spans(k):
+                nc.scalar.activation(
+                    roots[k][:, cols], mags[k][:, cols], ACT.Abs_reciprocal_sqrt, bias=floor[:, a, t : t + 1]
+                )
 
         def inverse(k):
             recips[k] = ring.tile([P, S], F32, name="recip", align_bytes=64)
-            nc.scalar.activation(recips[k][:], roots[k][:], ACT.Square)
+            for cols in spans(k):
+                nc.scalar.activation(recips[k][:, cols], roots[k][:, cols], ACT.Square)
 
         def limit(k):
             a, t = divmod(k, 4)
             bank = psum.tile([P, 512], F32, name="bank_t", tag="y")
             for jt in range(4):
                 nc.tensor.transpose(bank[:, P * jt : P * jt + P], clean[jt][:, a, t, :], ident[:])
-            ratio = ring.tile([P, S], F32, name="ratio", align_bytes=64)
-            nc.vector.tensor_tensor(ratio[:], bank[:], recips[k][:], ALU.mult)
-            return ratio
+            if k % 2 == 0:
+                ratios[k // 2] = ring.tile([P, 2, S], F32, name="ratio", align_bytes=64)
+            for cols in spans(k):
+                nc.vector.tensor_tensor(ratios[k // 2][:, k % 2, cols], bank[:, cols], recips[k][:, cols], ALU.mult)
 
-        def shrink(k, ratio):
+        def shrink(k):
             a, t = divmod(k, 4)
-            nc.vector.scalar_tensor_tensor(z_planes[a][:, t, :], ratio[:], 1.0, dirty[k][:], ALU.min, ALU.mult)
+            u = k // 2
+            if k >= last - 1:
+                for cols in spans(k):
+                    nc.vector.scalar_tensor_tensor(
+                        z_planes[a][:, t, cols], ratios[u][:, k % 2, cols], 1.0, dirty[u][:, k % 2, cols], ALU.min, ALU.mult
+                    )
+            elif k % 2 == 1:
+                nc.vector.scalar_tensor_tensor(
+                    z_planes[a][:, t - 1 : t + 1, :], ratios[u][:], 1.0, dirty[u][:], ALU.min, ALU.mult
+                )
 
-        def quant_z(a):
-            weave(z_bf[a][:], z_planes[a][:])
-            nc.vector.quantize_mx(out=z_codes[a][:].bitcast(E4M3), scales=z_sc[a][:], in_=z_bf[a][:])
+        z_codes = [kt("z_codes%d" % a, [P, S], U32) for a in range(2)]
+        z_sc = [kt("z_sc%d" % a, [P, S], U8) for a in range(2)]
+        banks = {}
 
-        ratios = {}
-        live = range(8)
-        for step in range(8 + 4):
-            if step in live:
-                project(step, 0)
-            if step - 2 in live:
-                inverse_root(step - 2)
-            if step - 3 in live:
-                ratios[step - 3] = limit(step - 3)
-            if step - 1 in live:
-                magnitude(step - 1)
-            if step in live:
-                project(step, 1)
-            if step - 2 in live:
-                inverse(step - 2)
-            if step in live:
-                pick(step)
-            if step - 3 in live:
-                shrink(step - 3, ratios[step - 3])
-            if step - 4 in (3, 7):
-                quant_z((step - 4) // 4)
-
-        banks = [psum.tile([P, 512], F32, name="bank_o", tag="x") for nt in range(4)]
-        for a in range(2):
+        def synth(a, h):
+            cols = slice(256 * h, 256 * h + 256)
             for nt in range(4):
+                if a == 0:
+                    banks[h, nt] = psum.tile([P, 256], F32, name="bank_o", tag="xy"[h])
                 nc.tensor.matmul_mx(
-                    out=banks[nt][:],
+                    out=banks[h, nt][:],
                     lhsT=wow[:, a, P * nt : P * nt + P].bitcast(E4M3),
                     lhsT_scale=wos[:, a, P * nt : P * nt + P],
-                    rhs=z_codes[a][:].bitcast(E4M3),
-                    rhs_scale=z_sc[a][:],
+                    rhs=z_codes[a][:, cols].bitcast(E4M3),
+                    rhs_scale=z_sc[a][:, cols],
                     start=(a == 0),
                     stop=(a == 1),
                 )
-        for nt in range(4):
-            res = kt("res%d" % nt, [P, S], F32)
-            if nt % 2 == 0:
-                nc.scalar.copy(res[:], banks[nt][:])
+                if a == 1:
+                    res = kt("res%d%d" % (h, nt), [P, 256], F32)
+                    copy = nc.scalar.copy if nt % 2 == 0 else nc.vector.tensor_copy
+                    copy(res[:], banks[h, nt][:])
+                    nc.sync.dma_start(out[P * nt : P * nt + P, cols], res[:])
+
+        def quant_z(a):
+            if a == 0:
+                z_bf = kt("z_bf0", [P, S, 4], BF16)
+                weave(z_bf[:], z_planes[0][:], 512)
+                quant(z_codes[0][:], z_sc[0][:], z_bf[:])
+                synth(0, 0)
             else:
-                nc.vector.tensor_copy(res[:], banks[nt][:])
-            nc.sync.dma_start(out[P * nt : P * nt + P, :], res[:])
+                synth(0, 1)
+                for h, cols in enumerate(spans(last)):
+                    z_bf = kt("z_bf1%d" % h, [P, 256, 4], BF16)
+                    weave(z_bf[:], z_planes[1][:, :, cols], 160)
+                    quant(z_codes[1][:, cols], z_sc[1][:, cols], z_bf[:])
+                    synth(1, h)
+
+        live = range(8)
+        lag_mag, lag_root, lag_limit = 4, 5, 6
+        for step in range(8 + lag_limit + 1):
+            if step in live:
+                project(step, 0)
+            if step - lag_root in live:
+                inverse_root(step - lag_root)
+            if step - lag_limit in live:
+                limit(step - lag_limit)
+            if step - lag_mag in live:
+                magnitude(step - lag_mag)
+            if step in live:
+                project(step, 1)
+            if step - lag_root in live:
+                inverse(step - lag_root)
+            if step in live:
+                pick(step)
+            if step - lag_limit in live:
+                shrink(step - lag_limit)
+            if step - lag_limit - 1 in (3, 7):
+                quant_z((step - lag_limit - 1) // 4)

@@ -74,8 +74,10 @@ def tile_list_chirp_interference_repair_kernel(
                     dram[:, 4 * q : 4 * q + 4, :].rearrange("a r c -> r a c").bitcast(I32),
                 )
 
-        def load_tab_scales():
-            load_scales(nc.sync, tabs, tab_scales)
+        def move_scales(q):
+            for a in range(2):
+                row = 16 * a + 4 * q
+                nc.sync.dma_start(vs[32 * q : 32 * q + 4, a, :].bitcast(I32), picked_rows[row : row + 4, :].bitcast(I32))
 
         def load_tab(a):
             nc.sync.dma_start(tabw[a][:], tab_words[a].rearrange("p t i -> p (t i)").bitcast(I32))
@@ -86,11 +88,16 @@ def tile_list_chirp_interference_repair_kernel(
         nc.sync.dma_start(tabs[0:32, :].bitcast(I32), tab_scales.rearrange("a q t -> (a q) t").bitcast(I32))
         nc.sync.dma_start(idx[:], offs)
         nc.sync.dma_start(idx2[:], offs2)
+        nc.vector.tensor_copy(picked_rows[:], tabs[:].indirect(idx[:]))
         load_plane(0)
         load_plane(1)
         load_tab(0)
         load_tab(1)
+        move_scales(0)
+        move_scales(1)
         load_plane(2)
+        move_scales(2)
+        move_scales(3)
         nc.sync.dma_start(w2w[:].bitcast(I32), w2_words.rearrange("a p c -> p a c").bitcast(I32))
         load_plane(3)
         load_w1(0)
@@ -168,11 +175,6 @@ def tile_list_chirp_interference_repair_kernel(
             for h in range(2):
                 quant(page_codes[h][:], page_sc[h][:], page_bf[h][:])
 
-        nc.vector.tensor_copy(picked_rows[:], tabs[:].indirect(idx[:]))
-        for a in range(2):
-            for q in range(4):
-                row = 16 * a + 4 * q
-                nc.scalar.dma_start(vs[32 * q : 32 * q + 4, a, :].bitcast(I32), picked_rows[row : row + 4, :].bitcast(I32))
         land(0)
         land(1)
         clean_path()

@@ -25,18 +25,19 @@ def tile_list_chirp_interference_repair_kernel(
     nc = tc.nc
     with ExitStack() as ctx:
         keep = ctx.enter_context(tc.tile_pool(name="keep", bufs=1))
-        ring = ctx.enter_context(tc.tile_pool(name="ring", bufs=3))
-        psum = ctx.enter_context(tc.psum_pool(name="psum", bufs=4))
+        ring = ctx.enter_context(tc.tile_pool(name="ring", bufs=2))
+        psum = ctx.enter_context(tc.psum_pool(name="psum", bufs=1))
 
         def kt(name, shape, dtype, tag=None):
             return keep.tile(shape, dtype, name=name, tag=tag or name, align_bytes=64)
 
+        psum_banks = [psum.tile([P, 512], F32, name="bank%d" % b) for b in range(8)]
         idx = keep.tile([P, S // 16], U16, name="idx")
         idx2 = keep.tile([P, S // 16], U16, name="idx2")
         idx3 = keep.tile([P, S // 16], U16, name="idx3")
         page = [kt("page%d" % i, [P, T2], F32) for i in range(4)]
         new = [kt("new%d" % i, [P, S], F32) for i in range(4)]
-        w1_raw = [kt("w1_raw%d" % a, [P, 4, 512], F32) for a in range(2)]
+        w1_raw = [kt("w1_raw%d" % g, [P, 4, 256], F32) for g in range(4)]
         tabw = [kt("tabw%d" % a, [P, T], I32) for a in range(2)]
         tabs = kt("tabs", [P, T], U8)
         picked_rows = kt("picked_rows", [P, S], U8)
@@ -77,241 +78,257 @@ def tile_list_chirp_interference_repair_kernel(
         def move_scales(q):
             for a in range(2):
                 row = 16 * a + 4 * q
-                nc.sync.dma_start(vs[32 * q : 32 * q + 4, a, :].bitcast(I32), picked_rows[row : row + 4, :].bitcast(I32))
+                nc.gpsimd.dma_start(vs[32 * q : 32 * q + 4, a, :].bitcast(I32), picked_rows[row : row + 4, :].bitcast(I32))
 
         def load_tab(a):
             nc.sync.dma_start(tabw[a][:], tab_words[a].rearrange("p t i -> p (t i)").bitcast(I32))
 
-        def load_w1(a):
-            nc.sync.dma_start(w1_raw[a][:], w1_rows[:, :, 512 * a : 512 * a + 512])
+        def load_w1(g):
+            nc.sync.dma_start(w1_raw[g][:], w1_rows[:, :, 256 * g : 256 * g + 256])
 
         nc.sync.dma_start(tabs[0:32, :].bitcast(I32), tab_scales.rearrange("a q t -> (a q) t").bitcast(I32))
         nc.sync.dma_start(idx[:], offs)
         nc.sync.dma_start(idx2[:], offs2)
         nc.vector.tensor_copy(picked_rows[:], tabs[:].indirect(idx[:]))
         load_plane(0)
+        load_w1(0)
         load_plane(1)
+        nc.sync.dma_start(idx3[:], offs3)
+        load_w1(1)
+        load_plane(2)
+        load_w1(2)
+        nc.sync.dma_start(floor[:], nf.rearrange("(a p t) -> p a t", a=2, t=4))
+        load_plane(3)
+        load_w1(3)
         load_tab(0)
         load_tab(1)
-        move_scales(0)
-        move_scales(1)
-        load_plane(2)
-        move_scales(2)
-        move_scales(3)
         nc.sync.dma_start(w2w[:].bitcast(I32), w2_words.rearrange("a p c -> p a c").bitcast(I32))
-        load_plane(3)
-        load_w1(0)
-        load_w1(1)
-        nc.sync.dma_start(idx3[:], offs3)
-        nc.sync.dma_start(floor[:], nf.rearrange("(a p t) -> p a t", a=2, t=4))
         load_scales(nc.gpsimd, w2s, w2_scales)
+        for q in range(4):
+            move_scales(q)
         nc.sync.dma_start(wow[:], wo_words.rearrange("a p n i -> p a (n i)").bitcast(I32))
         load_scales(nc.sync, wos, wo_scales)
 
-        page_planes = kt("page_planes", [P, 4, T2], BF16)
+        page_pairs = [kt("page_pairs%d" % h, [P, 2, 512, 2], BF16) for h in range(2)]
 
         def land(i):
             nc.vector.tensor_copy(page[i][:].indirect(idx2[:]), new[i][:])
-            if i < 3:
-                nc.gpsimd.tensor_scalar(page_planes[:, i, :], page[i][:], 1.0, 0.0, ALU.mult, ALU.add)
-            else:
-                for h in range(2):
-                    nc.vector.tensor_copy(page_planes[:, i, 512 * h : 512 * h + 512], page[i][:, 512 * h : 512 * h + 512])
+
+        def round_plane(i, h, copy):
+            copy(page_pairs[h][:, i // 2, :, i % 2], page[i][:, 512 * h : 512 * h + 512])
 
         w1_bf = [kt("w1_bf%d" % a, [P, 2048], BF16) for a in range(2)]
         w1_codes = {}
-        w1_sc = [kt("w1_sc%d" % a, [P, 512], U8) for a in range(2)]
+        w1_sc = {}
 
-        def round_w1(a):
+        def round_w1(g):
+            a, half = divmod(g, 2)
             dst = w1_bf[a][:].rearrange("p (t m j) -> p m j t", t=4, j=4)
-            src = w1_raw[a][:].rearrange("p j (m t) -> p m j t", t=4)
-            for m0 in range(0, P, 64):
-                nc.scalar.copy(dst[:, m0 : m0 + 64], src[:, m0 : m0 + 64])
+            nc.scalar.copy(dst[:, 64 * half : 64 * half + 64], w1_raw[g][:].rearrange("p j (m t) -> p m j t", t=4))
 
         def quant_w1(a):
-            w1_codes[a] = kt("w1_codes%d" % a, [P, 512], U32, tag="new%d" % (a + 2))
+            w1_codes[a] = kt("w1_codes%d" % a, [P, 512], U32, tag="new%d" % (3 - a))
+            w1_sc[a] = kt("w1_sc%d" % a, [P, 512], U8, tag="page%d" % (2 - a))
             nc.vector.quantize_mx(out=w1_codes[a][:].bitcast(E4M3), scales=w1_sc[a][:], in_=w1_bf[a][:])
 
-        clean = [kt("clean%d" % jt, [P, 2, 4, P], F32) for jt in range(4)]
+        def weave(woven, pairs):
+            nc.vector.tensor_copy(
+                woven.rearrange("p c t -> p (c t)").bitcast(I32).rearrange("p (c u) -> p c u", u=2),
+                pairs.rearrange("p u c e -> p u (c e)").bitcast(I32).rearrange("p u c -> p c u"),
+            )
 
-        def clean_path():
-            for a in range(2):
-                nc.vector.tensor_copy(vw[a][:], tabw[a][:].bitcast(U32).indirect(idx[:]))
-            for h in range(2):
-                for jt in range(4):
-                    bank = psum.tile([P, 512], F32, name="bank_b", tag="y")
-                    cols = slice(P * jt, P * jt + P)
-                    for a in range(2):
-                        nc.tensor.matmul_mx(
-                            out=bank[:],
-                            lhsT=vw[a][:, cols].bitcast(E4M3),
-                            lhsT_scale=vs[:, a, cols],
-                            rhs=w2w[:, a, 1024 * h : 1024 * h + 1024].bitcast(E2M1),
-                            rhs_scale=w2s[:, a, 512 * h : 512 * h + 512],
-                            start=(a == 0),
-                            stop=(a == 1),
-                        )
-                    nc.scalar.activation(clean[jt][:, h, :, :], bank[:].rearrange("p (m t) -> p t m", t=4), ACT.Abs)
+        def quant(codes, scales, woven):
+            nc.vector.quantize_mx(out=codes.bitcast(E4M3), scales=scales, in_=woven.rearrange("p c t -> p (c t)"))
 
         page_bf = [kt("page_bf%d" % h, [P, 512, 4], BF16) for h in range(2)]
         page_codes = [kt("page_codes%d" % h, [P, 512], U32) for h in range(2)]
         page_sc = [kt("page_sc%d" % h, [P, 512], U8) for h in range(2)]
 
-        def weave(dst, src, split):
-            width = dst.shape[1]
-            for copy, c0, c1 in ((nc.vector.tensor_copy, 0, split), (nc.scalar.copy, split, width)):
-                if c0 < c1:
-                    copy(
-                        dst[:, c0:c1, :].rearrange("p (c i) t -> p c t i", i=4),
-                        src[:, :, c0:c1].rearrange("p t (c i) -> p c t i", i=4),
-                    )
-
-        def quant(codes, scales, woven):
-            nc.vector.quantize_mx(out=codes.bitcast(E4M3), scales=scales, in_=woven.rearrange("p c t -> p (c t)"))
-
-        def quant_page():
-            for h in range(2):
-                weave(page_bf[h][:], page_planes[:, :, 512 * h : 512 * h + 512], 512)
-            for h in range(2):
-                quant(page_codes[h][:], page_sc[h][:], page_bf[h][:])
-
-        land(0)
-        land(1)
-        clean_path()
-        land(2)
+        for i in range(3):
+            land(i)
+            round_plane(i, 0, nc.scalar.copy)
+            round_plane(i, 1, nc.scalar.copy)
+            round_w1(i)
         land(3)
-        round_w1(0)
-        round_w1(1)
         quant_w1(0)
-        quant_page()
+        round_plane(3, 0, nc.vector.tensor_copy)
+        round_plane(3, 1, nc.scalar.copy)
+        round_w1(3)
+        for h in range(2):
+            weave(page_bf[h][:], page_pairs[h][:])
+        for h in range(2):
+            quant(page_codes[h][:], page_sc[h][:], page_bf[h][:])
+        for a in range(2):
+            nc.vector.tensor_copy(vw[a][:], tabw[a][:].bitcast(U32).indirect(idx[:]))
         quant_w1(1)
 
-        dirty = [kt("dirty%d" % u, [P, 2, S], F32) for u in range(4)]
-        z_planes = [kt("z_planes%d" % a, [P, 4, S], BF16) for a in range(2)]
-        projs = [kt("proj%d" % k, [P, T2], F32) for k in range(8)]
-        mags, roots, recips, ratios = {}, {}, {}, {}
-        last = 7
+        clean = [[kt("clean%d%d" % (a, jt), [P, 4, P], F32) for jt in range(4)] for a in range(2)]
 
-        def spans(k):
-            return [slice(0, 256), slice(256, 512)] if k == last else [slice(0, 512)]
-
-        def project(k, h):
-            a, t = divmod(k, 4)
-            bank = psum.tile([P, 512], F32, name="bank_a", tag="x")
-            nc.tensor.matmul_mx(
-                out=bank[:],
-                lhsT=w1_codes[a][:, P * t : P * t + P].bitcast(E4M3),
-                lhsT_scale=w1_sc[a][:, P * t : P * t + P],
-                rhs=page_codes[h][:].bitcast(E4M3),
-                rhs_scale=page_sc[h][:],
-                start=True,
-                stop=True,
-            )
-            copy = nc.vector.tensor_copy if (h == 1 and k < 2) else nc.scalar.copy
-            copy(projs[k][:, 512 * h : 512 * h + 512], bank[:])
-
-        def pick(k):
-            for cols in spans(k):
-                entries = idx3[:, cols.start // 16 : cols.stop // 16]
-                nc.vector.tensor_copy(dirty[k // 2][:, k % 2, cols], projs[k][:].indirect(entries))
-
-        def magnitude(k):
-            mags[k] = ring.tile([P, S], F32, name="mag", align_bytes=64)
-            for cols in spans(k):
-                nc.scalar.activation(mags[k][:, cols], dirty[k // 2][:, k % 2, cols], ACT.Abs)
-
-        def inverse_root(k):
-            a, t = divmod(k, 4)
-            roots[k] = ring.tile([P, S], F32, name="root", align_bytes=64)
-            for cols in spans(k):
-                nc.scalar.activation(
-                    roots[k][:, cols], mags[k][:, cols], ACT.Abs_reciprocal_sqrt, bias=floor[:, a, t : t + 1]
-                )
-
-        def inverse(k):
-            recips[k] = ring.tile([P, S], F32, name="recip", align_bytes=64)
-            for cols in spans(k):
-                nc.scalar.activation(recips[k][:, cols], roots[k][:, cols], ACT.Square)
-
-        def limit(k):
-            a, t = divmod(k, 4)
-            bank = psum.tile([P, 512], F32, name="bank_t", tag="y")
+        def clean_product(h, first_bank):
             for jt in range(4):
-                nc.tensor.transpose(bank[:, P * jt : P * jt + P], clean[jt][:, a, t, :], ident[:])
-            if k % 2 == 0:
-                ratios[k // 2] = ring.tile([P, 2, S], F32, name="ratio", align_bytes=64)
-            for cols in spans(k):
-                nc.vector.tensor_tensor(ratios[k // 2][:, k % 2, cols], bank[:, cols], recips[k][:, cols], ALU.mult)
-
-        def shrink(k):
-            a, t = divmod(k, 4)
-            u = k // 2
-            if k >= last - 1:
-                for cols in spans(k):
-                    nc.vector.scalar_tensor_tensor(
-                        z_planes[a][:, t, cols], ratios[u][:, k % 2, cols], 1.0, dirty[u][:, k % 2, cols], ALU.min, ALU.mult
+                bank = psum_banks[first_bank + jt]
+                cols = slice(P * jt, P * jt + P)
+                for a in range(2):
+                    nc.tensor.matmul_mx(
+                        out=bank[:],
+                        lhsT=vw[a][:, cols].bitcast(E4M3),
+                        lhsT_scale=vs[:, a, cols],
+                        rhs=w2w[:, a, 1024 * h : 1024 * h + 1024].bitcast(E2M1),
+                        rhs_scale=w2s[:, a, 512 * h : 512 * h + 512],
+                        start=(a == 0),
+                        stop=(a == 1),
                     )
-            elif k % 2 == 1:
-                nc.vector.scalar_tensor_tensor(
-                    z_planes[a][:, t - 1 : t + 1, :], ratios[u][:], 1.0, dirty[u][:], ALU.min, ALU.mult
+                nc.scalar.activation(clean[h][jt][:], bank[:].rearrange("p (m t) -> p t m", t=4), ACT.Abs)
+
+        recip_pairs = [kt("recip%d" % a, [P, 2, 2 * S], F32) for a in range(2)]
+        recips = [recip_pairs[u // 2][:, u % 2, :].rearrange("p (j e) -> p j e", e=2) for u in range(4)]
+        dirty = [kt("dirty%d" % u, [P, 2, S], F32)[:] for u in range(3)] + [recip_pairs[0][:, :, 0:S]]
+        z_pairs = [kt("z_pairs%d" % a, [P, 2, S, 2], BF16) for a in range(2)]
+        mags, roots, ratios, spread = {}, {}, {}, {}
+
+        def project(k, first_bank, engine_copies):
+            a, t = divmod(k, 4)
+            proj = kt("proj%d" % k, [P, T2], F32, tag={1: "tabw0", 4: "tabw1"}.get(k))
+            for h in range(2):
+                bank = psum_banks[first_bank + h]
+                nc.tensor.matmul_mx(
+                    out=bank[:],
+                    lhsT=w1_codes[a][:, P * t : P * t + P].bitcast(E4M3),
+                    lhsT_scale=w1_sc[a][:, P * t : P * t + P],
+                    rhs=page_codes[h][:].bitcast(E4M3),
+                    rhs_scale=page_sc[h][:],
+                    start=True,
+                    stop=True,
                 )
+                engine_copies[h](proj[:, 512 * h : 512 * h + 512], bank[:])
+            nc.vector.tensor_copy(dirty[k // 2][:, k % 2, :], proj[:].indirect(idx3[:]))
+
+        def inverse_root(u, cols):
+            if cols.start == 0:
+                mags[u] = ring.tile([P, 2, S], F32, name="mag", align_bytes=64)
+                roots[u] = ring.tile([P, 2, S], F32, name="root", align_bytes=64)
+            for e in range(2):
+                nc.scalar.activation(mags[u][:, e, cols], dirty[u][:, e, cols], ACT.Abs)
+            for e in range(2):
+                a, t = divmod(2 * u + e, 4)
+                nc.scalar.activation(
+                    roots[u][:, e, cols], mags[u][:, e, cols], ACT.Abs_reciprocal_sqrt, bias=floor[:, a, t : t + 1]
+                )
+
+        def inverse(u, cols):
+            nc.scalar.activation(recips[u][:, cols, :], roots[u][:, :, cols].rearrange("p e j -> p j e"), ACT.Square)
+
+        def turn_clean(u, first_bank):
+            for h in range(2):
+                bank = psum_banks[first_bank + h][:].rearrange("p (e j) -> p e j", e=2)
+                for e in range(2):
+                    for jj in range(2):
+                        nc.tensor.transpose(
+                            bank[:, e, P * jj : P * jj + P], clean[u // 2][2 * h + jj][:, 2 * (u % 2) + e, :], ident[:]
+                        )
+                spread[u, h] = bank.rearrange("p e j -> p j e")
+            ratios[u] = ring.tile([P, S, 2], F32, name="ratio", align_bytes=64)
+
+        def limit(u, cols):
+            h = cols.start // 256
+            inside = slice(cols.start - 256 * h, cols.stop - 256 * h)
+            nc.vector.tensor_tensor(ratios[u][:, cols, :], spread[u, h][:, inside, :], recips[u][:, cols, :], ALU.mult)
+
+        def shrink(u, cols):
+            nc.vector.scalar_tensor_tensor(
+                z_pairs[u // 2][:, u % 2, cols, :],
+                ratios[u][:, cols, :],
+                1.0,
+                dirty[u][:, :, cols].rearrange("p e j -> p j e"),
+                ALU.min,
+                ALU.mult,
+            )
 
         z_codes = [kt("z_codes%d" % a, [P, S], U32) for a in range(2)]
         z_sc = [kt("z_sc%d" % a, [P, S], U8) for a in range(2)]
-        banks = {}
+        out_rows = out.rearrange("(n p) j -> p n j", p=P)
+        z_bf = {}
 
-        def synth(a, h):
-            cols = slice(256 * h, 256 * h + 256)
-            for nt in range(4):
-                if a == 0:
-                    banks[h, nt] = psum.tile([P, 256], F32, name="bank_o", tag="xy"[h])
-                nc.tensor.matmul_mx(
-                    out=banks[h, nt][:],
-                    lhsT=wow[:, a, P * nt : P * nt + P].bitcast(E4M3),
-                    lhsT_scale=wos[:, a, P * nt : P * nt + P],
-                    rhs=z_codes[a][:, cols].bitcast(E4M3),
-                    rhs_scale=z_sc[a][:, cols],
-                    start=(a == 0),
-                    stop=(a == 1),
-                )
+        def weave_z(a, cols):
+            z_bf[a, cols.start] = kt("z_bf%d%d" % (a, cols.start), [P, cols.stop - cols.start, 4], BF16)
+            weave(z_bf[a, cols.start][:], z_pairs[a][:, :, cols, :])
+
+        def quant_z(a, cols):
+            quant(z_codes[a][:, cols], z_sc[a][:, cols], z_bf[a, cols.start][:])
+
+        def synth(a, cols, groups):
+            width = cols.stop - cols.start
+            for bank, tiles, copy in groups:
+                sums = psum_banks[bank][:, 0 : width * len(tiles)].rearrange("p (i j) -> p i j", j=width)
+                for i, nt in enumerate(tiles):
+                    nc.tensor.matmul_mx(
+                        out=sums[:, i, :],
+                        lhsT=wow[:, a, P * nt : P * nt + P].bitcast(E4M3),
+                        lhsT_scale=wos[:, a, P * nt : P * nt + P],
+                        rhs=z_codes[a][:, cols].bitcast(E4M3),
+                        rhs_scale=z_sc[a][:, cols],
+                        start=(a == 0 and i == 0),
+                        stop=(a == 1 and i == len(tiles) - 1),
+                    )
                 if a == 1:
-                    res = kt("res%d%d" % (h, nt), [P, 256], F32)
-                    copy = nc.scalar.copy if nt % 2 == 0 else nc.vector.tensor_copy
-                    copy(res[:], banks[h, nt][:])
-                    nc.sync.dma_start(out[P * nt : P * nt + P, cols], res[:])
+                    res = kt("res%d" % bank, [P, len(tiles), width], F32)
+                    copy(res[:], sums)
+                    nc.sync.dma_start(out_rows[:, tiles[0] : tiles[-1] + 1, cols], res[:])
 
-        def quant_z(a):
-            if a == 0:
-                z_bf = kt("z_bf0", [P, S, 4], BF16)
-                weave(z_bf[:], z_planes[0][:], 512)
-                quant(z_codes[0][:], z_sc[0][:], z_bf[:])
-                synth(0, 0)
-            else:
-                synth(0, 1)
-                for h, cols in enumerate(spans(last)):
-                    z_bf = kt("z_bf1%d" % h, [P, 256, 4], BF16)
-                    weave(z_bf[:], z_planes[1][:, :, cols], 160)
-                    quant(z_codes[1][:, cols], z_sc[1][:, cols], z_bf[:])
-                    synth(1, h)
+        whole = slice(0, S)
+        halves = [slice(0, 256), slice(256, 512)]
+        scalar, vector = nc.scalar.copy, nc.vector.tensor_copy
+        pieces = [
+            (slice(0, 256), [(3, [0, 1], scalar), (4, [2, 3], scalar)]),
+            (slice(256, 384), [(5, [0, 1, 2, 3], scalar)]),
+            (slice(384, 512), [(6, [0, 1], scalar), (7, [2, 3], vector)]),
+        ]
 
-        live = range(8)
-        lag_mag, lag_root, lag_limit = 4, 5, 6
-        for step in range(8 + lag_limit + 1):
-            if step in live:
-                project(step, 0)
-            if step - lag_root in live:
-                inverse_root(step - lag_root)
-            if step - lag_limit in live:
-                limit(step - lag_limit)
-            if step - lag_mag in live:
-                magnitude(step - lag_mag)
-            if step in live:
-                project(step, 1)
-            if step - lag_root in live:
-                inverse(step - lag_root)
-            if step in live:
-                pick(step)
-            if step - lag_limit in live:
-                shrink(step - lag_limit)
-            if step - lag_limit - 1 in (3, 7):
-                quant_z((step - lag_limit - 1) // 4)
+        def finish(u):
+            for cols in halves:
+                limit(u, cols)
+            shrink(u, whole)
+
+        project(0, 0, (scalar, scalar))
+        project(1, 2, (vector, vector))
+        project(2, 4, (scalar, scalar))
+        project(3, 6, (scalar, scalar))
+        project(5, 0, (scalar, scalar))
+        inverse_root(0, whole)
+        inverse(0, whole)
+        project(4, 2, (vector, vector))
+        clean_product(0, 4)
+        turn_clean(0, 0)
+        finish(0)
+        turn_clean(1, 2)
+        inverse_root(1, whole)
+        inverse(1, whole)
+        project(6, 0, (vector, scalar))
+        for cols in halves:
+            limit(1, cols)
+        project(7, 4, (scalar, scalar))
+        shrink(1, whole)
+        clean_product(1, 4)
+        for cols in halves:
+            weave_z(0, cols)
+        for cols in halves:
+            quant_z(0, cols)
+        turn_clean(2, 0)
+        for cols, groups in pieces:
+            synth(0, cols, groups)
+        for cols in halves:
+            inverse_root(2, cols)
+            inverse(2, cols)
+        for cols in halves:
+            limit(2, cols)
+        for cols in halves:
+            shrink(2, cols)
+        turn_clean(3, 1)
+        for cols, groups in pieces:
+            inverse_root(3, cols)
+            inverse(3, cols)
+            limit(3, cols)
+            shrink(3, cols)
+            weave_z(1, cols)
+            quant_z(1, cols)
+            synth(1, cols, groups)

@@ -51,6 +51,7 @@ def tile_list_chirp_interference_repair_kernel(
         ident = kt("ident", [P, P], F32)
         warm = kt("warm", [P, 8], F32)
 
+        nc.scalar.dma_start(tabs[0:32, :].bitcast(I32), tab_scales.rearrange("a q t -> (a q) t").bitcast(I32))
         nc.gpsimd.memset(warm[:], 1.0)
         nc.scalar.activation(warm[:, 4:5], warm[:, 0:1], ACT.Abs_reciprocal_sqrt)
         nc.vector.memset(tabs[32:64, :].bitcast(I32), 0)
@@ -78,7 +79,7 @@ def tile_list_chirp_interference_repair_kernel(
         def move_scales(q):
             for a in range(2):
                 row = 16 * a + 4 * q
-                nc.gpsimd.dma_start(vs[32 * q : 32 * q + 4, a, :].bitcast(I32), picked_rows[row : row + 4, :].bitcast(I32))
+                nc.sync.dma_start(vs[32 * q : 32 * q + 4, a, :].bitcast(I32), picked_rows[row : row + 4, :].bitcast(I32))
 
         def load_tab(a):
             nc.sync.dma_start(tabw[a][:], tab_words[a].rearrange("p t i -> p (t i)").bitcast(I32))
@@ -86,7 +87,6 @@ def tile_list_chirp_interference_repair_kernel(
         def load_w1(g):
             nc.sync.dma_start(w1_raw[g][:], w1_rows[:, :, 256 * g : 256 * g + 256])
 
-        nc.sync.dma_start(tabs[0:32, :].bitcast(I32), tab_scales.rearrange("a q t -> (a q) t").bitcast(I32))
         nc.sync.dma_start(idx[:], offs)
         nc.sync.dma_start(idx2[:], offs2)
         nc.vector.tensor_copy(picked_rows[:], tabs[:].indirect(idx[:]))
@@ -164,9 +164,9 @@ def tile_list_chirp_interference_repair_kernel(
 
         clean = [[kt("clean%d%d" % (a, jt), [P, 4, P], F32) for jt in range(4)] for a in range(2)]
 
-        def clean_product(h, first_bank):
+        def clean_product(h, bank_numbers):
             for jt in range(4):
-                bank = psum_banks[first_bank + jt]
+                bank = psum_banks[bank_numbers[jt]]
                 cols = slice(P * jt, P * jt + P)
                 for a in range(2):
                     nc.tensor.matmul_mx(
@@ -182,15 +182,19 @@ def tile_list_chirp_interference_repair_kernel(
 
         recip_pairs = [kt("recip%d" % a, [P, 2, 2 * S], F32) for a in range(2)]
         recips = [recip_pairs[u // 2][:, u % 2, :].rearrange("p (j e) -> p j e", e=2) for u in range(4)]
-        dirty = [kt("dirty%d" % u, [P, 2, S], F32)[:] for u in range(3)] + [recip_pairs[0][:, :, 0:S]]
+        dirty_pairs = [kt("dirty%d" % a, [P, 2, 2, S], F32, tag=("tabw1" if a == 0 else None)) for a in range(2)]
+        dirty = [dirty_pairs[u // 2][:, u % 2, :, :] for u in range(4)]
         z_pairs = [kt("z_pairs%d" % a, [P, 2, S, 2], BF16) for a in range(2)]
-        mags, roots, ratios, spread = {}, {}, {}, {}
+        root_pairs = [kt("root%d" % a, [P, 2, 2, S], F32) for a in range(2)]
+        roots = [root_pairs[u // 2][:, u % 2, :, :] for u in range(4)]
+        mag_pairs = [kt("mag%d" % a, [P, 2, 2, S], F32) for a in range(2)]
+        ratios, spread = {}, {}
 
-        def project(k, first_bank, engine_copies):
+        def project(k, bank_numbers, engine_copies):
             a, t = divmod(k, 4)
-            proj = kt("proj%d" % k, [P, T2], F32, tag={1: "tabw0", 4: "tabw1"}.get(k))
+            proj = kt("proj%d" % k, [P, T2], F32, tag={1: "tabw0", 5: "w1_raw2", 6: "w1_raw0", 7: "w1_raw1"}.get(k))
             for h in range(2):
-                bank = psum_banks[first_bank + h]
+                bank = psum_banks[bank_numbers[h]]
                 nc.tensor.matmul_mx(
                     out=bank[:],
                     lhsT=w1_codes[a][:, P * t : P * t + P].bitcast(E4M3),
@@ -203,33 +207,42 @@ def tile_list_chirp_interference_repair_kernel(
                 engine_copies[h](proj[:, 512 * h : 512 * h + 512], bank[:])
             nc.vector.tensor_copy(dirty[k // 2][:, k % 2, :], proj[:].indirect(idx3[:]))
 
-        def inverse_root(u, cols):
-            if cols.start == 0:
-                mags[u] = ring.tile([P, 2, S], F32, name="mag", align_bytes=64)
-                roots[u] = ring.tile([P, 2, S], F32, name="root", align_bytes=64)
+        def inverse_root(pairs, cols):
+            a = pairs[0] // 2
             for e in range(2):
-                nc.scalar.activation(mags[u][:, e, cols], dirty[u][:, e, cols], ACT.Abs)
+                us = slice(pairs[0] % 2, pairs[-1] % 2 + 1)
+                nc.scalar.activation(mag_pairs[a][:, us, e, cols], dirty_pairs[a][:, us, e, cols], ACT.Abs)
             for e in range(2):
-                a, t = divmod(2 * u + e, 4)
-                nc.scalar.activation(
-                    roots[u][:, e, cols], mags[u][:, e, cols], ACT.Abs_reciprocal_sqrt, bias=floor[:, a, t : t + 1]
-                )
+                for u in pairs:
+                    t = 2 * (u % 2) + e
+                    nc.scalar.activation(
+                        roots[u][:, e, cols],
+                        mag_pairs[a][:, u % 2, e, cols],
+                        ACT.Abs_reciprocal_sqrt,
+                        bias=floor[:, a, t : t + 1],
+                    )
 
-        def inverse(u, cols):
-            nc.scalar.activation(recips[u][:, cols, :], roots[u][:, :, cols].rearrange("p e j -> p j e"), ACT.Square)
+        def inverse(pairs, cols):
+            a = pairs[0] // 2
+            us = slice(pairs[0] % 2, pairs[-1] % 2 + 1)
+            nc.scalar.activation(
+                recip_pairs[a][:, us, :].rearrange("p u (j e) -> p u j e", e=2)[:, :, cols, :],
+                root_pairs[a][:, us, :, cols].rearrange("p u e j -> p u j e"),
+                ACT.Square,
+            )
 
-        def turn_clean(u, first_bank):
-            for h in range(2):
-                bank = psum_banks[first_bank + h][:].rearrange("p (e j) -> p e j", e=2)
-                for e in range(2):
-                    for jj in range(2):
-                        nc.tensor.transpose(
-                            bank[:, e, P * jj : P * jj + P], clean[u // 2][2 * h + jj][:, 2 * (u % 2) + e, :], ident[:]
-                        )
-                spread[u, h] = bank.rearrange("p e j -> p j e")
-            ratios[u] = ring.tile([P, S, 2], F32, name="ratio", align_bytes=64)
+        def turn_clean(u, h, bank_number):
+            bank = psum_banks[bank_number][:].rearrange("p (e j) -> p e j", e=2)
+            for e in range(2):
+                for jj in range(2):
+                    nc.tensor.transpose(
+                        bank[:, e, P * jj : P * jj + P], clean[u // 2][2 * h + jj][:, 2 * (u % 2) + e, :], ident[:]
+                    )
+            spread[u, h] = bank.rearrange("p e j -> p j e")
 
         def limit(u, cols):
+            if cols.start == 0:
+                ratios[u] = ring.tile([P, S, 2], F32, name="ratio", align_bytes=64)
             h = cols.start // 256
             inside = slice(cols.start - 256 * h, cols.stop - 256 * h)
             nc.vector.tensor_tensor(ratios[u][:, cols, :], spread[u, h][:, inside, :], recips[u][:, cols, :], ALU.mult)
@@ -279,56 +292,62 @@ def tile_list_chirp_interference_repair_kernel(
         halves = [slice(0, 256), slice(256, 512)]
         scalar, vector = nc.scalar.copy, nc.vector.tensor_copy
         pieces = [
-            (slice(0, 256), [(3, [0, 1], scalar), (4, [2, 3], scalar)]),
-            (slice(256, 384), [(5, [0, 1, 2, 3], scalar)]),
-            (slice(384, 512), [(6, [0, 1], scalar), (7, [2, 3], vector)]),
+            (slice(0, 256), [(4, [0, 1], scalar), (3, [2, 3], scalar)]),
+            (slice(256, 384), [(0, [0, 1, 2, 3], scalar)]),
+            (slice(384, 512), [(1, [0, 1], scalar), (2, [2, 3], vector)]),
         ]
 
         def finish(u):
             for cols in halves:
                 limit(u, cols)
-            shrink(u, whole)
+            for cols in halves:
+                shrink(u, cols)
 
-        project(0, 0, (scalar, scalar))
-        project(1, 2, (vector, vector))
-        project(2, 4, (scalar, scalar))
-        project(3, 6, (scalar, scalar))
-        project(5, 0, (scalar, scalar))
-        inverse_root(0, whole)
-        inverse(0, whole)
-        project(4, 2, (vector, vector))
-        clean_product(0, 4)
-        turn_clean(0, 0)
-        finish(0)
-        turn_clean(1, 2)
-        inverse_root(1, whole)
-        inverse(1, whole)
-        project(6, 0, (vector, scalar))
-        for cols in halves:
-            limit(1, cols)
-        project(7, 4, (scalar, scalar))
-        shrink(1, whole)
-        clean_product(1, 4)
+        project(0, (0, 1), (scalar, scalar))
+        project(1, (2, 3), (vector, vector))
+        project(2, (4, 5), (scalar, scalar))
+        project(3, (6, 7), (scalar, scalar))
+        project(5, (0, 1), (scalar, scalar))
+        project(6, (2, 3), (scalar, scalar))
+        project(4, (0, 1), (vector, vector))
+        project(7, (4, 3), (scalar, scalar))
+        clean_product(0, (6, 7, 5, 2))
+        turn_clean(0, 0, 6)
+        turn_clean(0, 1, 7)
+        turn_clean(1, 0, 5)
+        turn_clean(1, 1, 2)
+        for u in range(2):
+            inverse_root([u], whole)
+            inverse([u], whole)
+            finish(u)
+        clean_product(1, (4, 3, 0, 1))
         for cols in halves:
             weave_z(0, cols)
         for cols in halves:
             quant_z(0, cols)
-        turn_clean(2, 0)
+        turn_clean(2, 0, 6)
+        turn_clean(3, 0, 7)
+        turn_clean(2, 1, 5)
         for cols, groups in pieces:
             synth(0, cols, groups)
-        for cols in halves:
-            inverse_root(2, cols)
-            inverse(2, cols)
-        for cols in halves:
-            limit(2, cols)
-        for cols in halves:
-            shrink(2, cols)
-        turn_clean(3, 1)
-        for cols, groups in pieces:
-            inverse_root(3, cols)
-            inverse(3, cols)
-            limit(3, cols)
-            shrink(3, cols)
+
+        def leave(cols, groups):
             weave_z(1, cols)
             quant_z(1, cols)
             synth(1, cols, groups)
+
+        for u in (2, 3):
+            inverse_root([u], halves[0])
+            inverse([u], halves[0])
+            limit(u, halves[0])
+            shrink(u, halves[0])
+        leave(*pieces[0])
+        turn_clean(3, 1, 6)
+        for cols, groups in pieces[1:]:
+            inverse_root([2, 3], cols)
+            inverse([2, 3], cols)
+            for u in (2, 3):
+                limit(u, cols)
+            for u in (2, 3):
+                shrink(u, cols)
+            leave(cols, groups)

@@ -165,7 +165,7 @@ def tile_list_chirp_interference_repair_kernel(
         clean = [[kt("clean%d%d" % (a, jt), [P, 4, P], F32) for jt in range(4)] for a in range(2)]
 
         def clean_product(h, bank_numbers):
-            for jt in range(4):
+            for jt in (0, 2, 1, 3):
                 bank = psum_banks[bank_numbers[jt]]
                 cols = slice(P * jt, P * jt + P)
                 for a in range(2):
@@ -182,17 +182,17 @@ def tile_list_chirp_interference_repair_kernel(
 
         recip_pairs = [kt("recip%d" % a, [P, 2, 2 * S], F32) for a in range(2)]
         recips = [recip_pairs[u // 2][:, u % 2, :].rearrange("p (j e) -> p j e", e=2) for u in range(4)]
-        dirty_pairs = [kt("dirty%d" % a, [P, 2, 2, S], F32, tag=("tabw1" if a == 0 else None)) for a in range(2)]
+        dirty_pairs = [kt("dirty%d" % a, [P, 2, 2, S], F32) for a in range(2)]
         dirty = [dirty_pairs[u // 2][:, u % 2, :, :] for u in range(4)]
         z_pairs = [kt("z_pairs%d" % a, [P, 2, S, 2], BF16) for a in range(2)]
         root_pairs = [kt("root%d" % a, [P, 2, 2, S], F32) for a in range(2)]
         roots = [root_pairs[u // 2][:, u % 2, :, :] for u in range(4)]
-        mag_pairs = [kt("mag%d" % a, [P, 2, 2, S], F32) for a in range(2)]
+        mag_pairs = [kt("mag%d" % a, [P, 2, 2, S], F32, tag="mag") for a in range(2)]
         ratios, spread = {}, {}
 
         def project(k, bank_numbers, engine_copies):
             a, t = divmod(k, 4)
-            proj = kt("proj%d" % k, [P, T2], F32, tag={1: "tabw0", 5: "w1_raw2", 6: "w1_raw0", 7: "w1_raw1"}.get(k))
+            proj = kt("proj%d" % k, [P, T2], F32, tag={5: "w1_raw2", 6: "w1_raw0", 7: "w1_raw1"}.get(k))
             for h in range(2):
                 bank = psum_banks[bank_numbers[h]]
                 nc.tensor.matmul_mx(
@@ -207,20 +207,18 @@ def tile_list_chirp_interference_repair_kernel(
                 engine_copies[h](proj[:, 512 * h : 512 * h + 512], bank[:])
             nc.vector.tensor_copy(dirty[k // 2][:, k % 2, :], proj[:].indirect(idx3[:]))
 
-        def inverse_root(pairs, cols):
-            a = pairs[0] // 2
+        def magnitude(u, planes, cols):
+            nc.scalar.activation(mag_pairs[u // 2][:, u % 2, planes, cols], dirty[u][:, planes, cols], ACT.Abs)
+
+        def inverse_root(u, cols):
             for e in range(2):
-                us = slice(pairs[0] % 2, pairs[-1] % 2 + 1)
-                nc.scalar.activation(mag_pairs[a][:, us, e, cols], dirty_pairs[a][:, us, e, cols], ACT.Abs)
-            for e in range(2):
-                for u in pairs:
-                    t = 2 * (u % 2) + e
-                    nc.scalar.activation(
-                        roots[u][:, e, cols],
-                        mag_pairs[a][:, u % 2, e, cols],
-                        ACT.Abs_reciprocal_sqrt,
-                        bias=floor[:, a, t : t + 1],
-                    )
+                a, t = divmod(2 * u + e, 4)
+                nc.scalar.activation(
+                    roots[u][:, e, cols],
+                    mag_pairs[a][:, u % 2, e, cols],
+                    ACT.Abs_reciprocal_sqrt,
+                    bias=floor[:, a, t : t + 1],
+                )
 
         def inverse(pairs, cols):
             a = pairs[0] // 2
@@ -306,7 +304,7 @@ def tile_list_chirp_interference_repair_kernel(
         project(0, (0, 1), (scalar, scalar))
         project(1, (2, 3), (vector, vector))
         project(2, (4, 5), (scalar, scalar))
-        project(3, (6, 7), (scalar, scalar))
+        project(3, (6, 7), (scalar, vector))
         project(5, (0, 1), (scalar, scalar))
         project(6, (2, 3), (scalar, scalar))
         project(4, (0, 1), (vector, vector))
@@ -317,7 +315,9 @@ def tile_list_chirp_interference_repair_kernel(
         turn_clean(1, 0, 5)
         turn_clean(1, 1, 2)
         for u in range(2):
-            inverse_root([u], whole)
+            for e in range(2):
+                magnitude(u, slice(e, e + 1), whole)
+            inverse_root(u, whole)
             inverse([u], whole)
             finish(u)
         clean_product(1, (4, 3, 0, 1))
@@ -337,17 +337,20 @@ def tile_list_chirp_interference_repair_kernel(
             synth(1, cols, groups)
 
         for u in (2, 3):
-            inverse_root([u], halves[0])
+            magnitude(u, slice(0, 2), halves[0])
+        for u in (2, 3):
+            inverse_root(u, halves[0])
             inverse([u], halves[0])
             limit(u, halves[0])
             shrink(u, halves[0])
         leave(*pieces[0])
         turn_clean(3, 1, 6)
         for cols, groups in pieces[1:]:
-            inverse_root([2, 3], cols)
-            inverse([2, 3], cols)
             for u in (2, 3):
+                magnitude(u, slice(0, 2), cols)
+            for u in (2, 3):
+                inverse_root(u, cols)
+                inverse([u], cols)
                 limit(u, cols)
-            for u in (2, 3):
                 shrink(u, cols)
             leave(cols, groups)

@@ -151,6 +151,16 @@ def tile_list_chirp_interference_repair_kernel(
             round_w1(i)
         land(3)
         quant_w1(0)
+        for b in range(3):
+            nc.tensor.matmul_mx(
+                out=psum_banks[5 + b][:],
+                lhsT=w1_codes[0][:, 0:P].bitcast(E4M3),
+                lhsT_scale=w1_sc[0][:, 0:P],
+                rhs=w1_codes[0][:].bitcast(E4M3),
+                rhs_scale=w1_sc[0][:],
+                start=True,
+                stop=True,
+            )
         round_plane(3, 0, nc.vector.tensor_copy)
         round_plane(3, 1, nc.scalar.copy)
         round_w1(3)

@@ -102,10 +102,10 @@ def tile_list_chirp_interference_repair_kernel(
         load_w1(3)
         load_tab(0)
         load_tab(1)
-        nc.sync.dma_start(w2w[:].bitcast(I32), w2_words.rearrange("a p c -> p a c").bitcast(I32))
-        load_scales(nc.gpsimd, w2s, w2_scales)
         for q in range(4):
             move_scales(q)
+        nc.sync.dma_start(w2w[:].bitcast(I32), w2_words.rearrange("a p c -> p a c").bitcast(I32))
+        load_scales(nc.gpsimd, w2s, w2_scales)
         nc.sync.dma_start(wow[:], wo_words.rearrange("a p n i -> p a (n i)").bitcast(I32))
         load_scales(nc.sync, wos, wo_scales)
 
@@ -174,8 +174,8 @@ def tile_list_chirp_interference_repair_kernel(
 
         clean = [[kt("clean%d%d" % (a, jt), [P, 4, P], F32) for jt in range(4)] for a in range(2)]
 
-        def clean_product(h, bank_numbers):
-            for jt in (0, 2, 1, 3):
+        def clean_product(h, column_tiles, bank_numbers):
+            for jt in column_tiles:
                 bank = psum_banks[bank_numbers[jt]]
                 cols = slice(P * jt, P * jt + P)
                 for a in range(2):
@@ -188,11 +188,18 @@ def tile_list_chirp_interference_repair_kernel(
                         start=(a == 0),
                         stop=(a == 1),
                     )
+
+        def clean_magnitude(h, column_tiles, bank_numbers):
+            for jt in column_tiles:
+                bank = psum_banks[bank_numbers[jt]]
                 nc.scalar.activation(clean[h][jt][:], bank[:].rearrange("p (m t) -> p t m", t=4), ACT.Abs)
 
         recip_pairs = [kt("recip%d" % a, [P, 2, 2 * S], F32) for a in range(2)]
         recips = [recip_pairs[u // 2][:, u % 2, :].rearrange("p (j e) -> p j e", e=2) for u in range(4)]
-        dirty_pairs = [kt("dirty%d" % a, [P, 2, 2, S], F32) for a in range(2)]
+        after_table = kt("after_table", [P, 5, T2], F32, tag="picked_rows")
+        dirty_pairs = [
+            after_table[:, 2 * a : 2 * a + 2, :].rearrange("p u (e j) -> p u e j", e=2) for a in range(2)
+        ]
         dirty = [dirty_pairs[u // 2][:, u % 2, :, :] for u in range(4)]
         z_pairs = [kt("z_pairs%d" % a, [P, 2, S, 2], BF16) for a in range(2)]
         root_pairs = [kt("root%d" % a, [P, 2, 2, S], F32) for a in range(2)]
@@ -200,9 +207,14 @@ def tile_list_chirp_interference_repair_kernel(
         mag_pairs = [kt("mag%d" % a, [P, 2, 2, S], F32, tag="mag") for a in range(2)]
         ratios, spread = {}, {}
 
+        projs = {}
+
         def project(k, bank_numbers, engine_copies):
             a, t = divmod(k, 4)
-            proj = kt("proj%d" % k, [P, T2], F32, tag={5: "w1_raw2", 6: "w1_raw0", 7: "w1_raw1"}.get(k))
+            if k == 4:
+                projs[k] = after_table[:, 4, :]
+            else:
+                projs[k] = kt("proj%d" % k, [P, T2], F32, tag={5: "w1_raw2", 6: "w1_raw0", 7: "w1_raw1"}.get(k))[:]
             for h in range(2):
                 bank = psum_banks[bank_numbers[h]]
                 nc.tensor.matmul_mx(
@@ -214,8 +226,10 @@ def tile_list_chirp_interference_repair_kernel(
                     start=True,
                     stop=True,
                 )
-                engine_copies[h](proj[:, 512 * h : 512 * h + 512], bank[:])
-            nc.vector.tensor_copy(dirty[k // 2][:, k % 2, :], proj[:].indirect(idx3[:]))
+                engine_copies[h](projs[k][:, 512 * h : 512 * h + 512], bank[:])
+
+        def pick(k):
+            nc.vector.tensor_copy(dirty[k // 2][:, k % 2, :], projs[k].indirect(idx3[:]))
 
         def magnitude(u, planes, cols):
             nc.scalar.activation(mag_pairs[u // 2][:, u % 2, planes, cols], dirty[u][:, planes, cols], ACT.Abs)
@@ -300,9 +314,9 @@ def tile_list_chirp_interference_repair_kernel(
         halves = [slice(0, 256), slice(256, 512)]
         scalar, vector = nc.scalar.copy, nc.vector.tensor_copy
         pieces = [
-            (slice(0, 256), [(4, [0, 1], scalar), (3, [2, 3], scalar)]),
-            (slice(256, 384), [(0, [0, 1, 2, 3], scalar)]),
-            (slice(384, 512), [(1, [0, 1], scalar), (2, [2, 3], vector)]),
+            (slice(0, 256), [(6, [0, 1], scalar), (2, [2, 3], scalar)]),
+            (slice(256, 384), [(4, [0, 1, 2, 3], scalar)]),
+            (slice(384, 512), [(3, [0, 1], scalar), (7, [2, 3], vector)]),
         ]
 
         def finish(u):
@@ -316,29 +330,36 @@ def tile_list_chirp_interference_repair_kernel(
         project(2, (4, 5), (scalar, scalar))
         project(3, (6, 7), (scalar, vector))
         project(5, (0, 1), (scalar, scalar))
-        project(6, (2, 3), (scalar, scalar))
+        project(6, (4, 5), (scalar, scalar))
+        project(7, (6, 2), (scalar, scalar))
+        pick(0)
+        pick(1)
         project(4, (0, 1), (vector, vector))
-        project(7, (4, 3), (scalar, scalar))
-        clean_product(0, (6, 7, 5, 2))
-        turn_clean(0, 0, 6)
-        turn_clean(0, 1, 7)
-        turn_clean(1, 0, 5)
-        turn_clean(1, 1, 2)
+        for k in range(2, 8):
+            pick(k)
+        clean_product(0, (0, 2, 1, 3), (3, 4, 7, 5))
+        clean_product(1, (0, 2), (6, 4, 2, 5))
+        clean_magnitude(0, (0, 2, 1, 3), (3, 4, 7, 5))
+        turn_clean(0, 0, 0)
+        turn_clean(0, 1, 1)
+        turn_clean(1, 0, 3)
+        turn_clean(1, 1, 7)
         for u in range(2):
             for e in range(2):
                 magnitude(u, slice(e, e + 1), whole)
             inverse_root(u, whole)
             inverse([u], whole)
             finish(u)
-        clean_product(1, (4, 3, 0, 1))
+        clean_product(1, (1, 3), (6, 4, 2, 5))
+        clean_magnitude(1, (0, 2, 1, 3), (6, 4, 2, 5))
         for cols in halves:
             weave_z(0, cols)
         for cols in halves:
             quant_z(0, cols)
-        turn_clean(2, 0, 6)
-        turn_clean(3, 0, 7)
-        turn_clean(2, 1, 5)
-        for cols, groups in pieces:
+        turn_clean(2, 0, 0)
+        turn_clean(3, 0, 1)
+        turn_clean(2, 1, 3)
+        for cols, groups in pieces[:2]:
             synth(0, cols, groups)
 
         def leave(cols, groups):
@@ -354,7 +375,7 @@ def tile_list_chirp_interference_repair_kernel(
             limit(u, halves[0])
             shrink(u, halves[0])
         leave(*pieces[0])
-        turn_clean(3, 1, 6)
+        turn_clean(3, 1, 7)
         for cols, groups in pieces[1:]:
             for u in (2, 3):
                 magnitude(u, slice(0, 2), cols)
@@ -363,4 +384,6 @@ def tile_list_chirp_interference_repair_kernel(
                 inverse([u], cols)
                 limit(u, cols)
                 shrink(u, cols)
+            if cols.stop == S:
+                synth(0, cols, groups)
             leave(cols, groups)

@@ -328,27 +328,31 @@ def tile_list_chirp_interference_repair_kernel(
         project(0, (0, 1), (scalar, scalar))
         project(1, (2, 3), (vector, vector))
         project(2, (4, 5), (scalar, scalar))
-        project(3, (6, 7), (scalar, vector))
+        project(3, (6, 7), (scalar, scalar))
         project(5, (0, 1), (scalar, scalar))
         project(6, (4, 5), (scalar, scalar))
         project(7, (6, 2), (scalar, scalar))
-        pick(0)
-        pick(1)
+        for k in range(4):
+            pick(k)
         project(4, (0, 1), (vector, vector))
-        for k in range(2, 8):
+        for k in range(4, 8):
             pick(k)
         clean_product(0, (0, 2, 1, 3), (3, 4, 7, 5))
         clean_product(1, (0, 2), (6, 4, 2, 5))
+        for u in range(2):
+            for e in range(2):
+                magnitude(u, slice(e, e + 1), whole)
+            inverse_root(u, whole)
+            planar = recip_pairs[0][:, u, :].rearrange("p (e j) -> p e j", e=2)
+            for e in range(2):
+                nc.gpsimd.tensor_tensor(planar[:, e, :], roots[u][:, e, :], roots[u][:, e, :], ALU.mult)
+            recips[u] = planar.rearrange("p e j -> p j e")
         clean_magnitude(0, (0, 2, 1, 3), (3, 4, 7, 5))
         turn_clean(0, 0, 0)
         turn_clean(0, 1, 1)
         turn_clean(1, 0, 3)
         turn_clean(1, 1, 7)
         for u in range(2):
-            for e in range(2):
-                magnitude(u, slice(e, e + 1), whole)
-            inverse_root(u, whole)
-            inverse([u], whole)
             finish(u)
         clean_product(1, (1, 3), (6, 4, 2, 5))
         clean_magnitude(1, (0, 2, 1, 3), (6, 4, 2, 5))

@@ -140,7 +140,7 @@ def tile_list_chirp_interference_repair_kernel(
         def quant(codes, scales, woven):
             nc.vector.quantize_mx(out=codes.bitcast(E4M3), scales=scales, in_=woven.rearrange("p c t -> p (c t)"))
 
-        page_bf = [kt("page_bf%d" % h, [P, 512, 4], BF16) for h in range(2)]
+        page_bf = [{c: kt("page_bf%d_%d" % (h, c), [P, 256, 4], BF16) for c in (0, 256)} for h in range(2)]
         page_codes = [kt("page_codes%d" % h, [P, 512], U32) for h in range(2)]
         page_sc = [kt("page_sc%d" % h, [P, 512], U8) for h in range(2)]
 
@@ -151,9 +151,9 @@ def tile_list_chirp_interference_repair_kernel(
             round_w1(i)
         land(3)
         quant_w1(0)
-        for b in range(3):
+        for b in range(2):
             nc.tensor.matmul_mx(
-                out=psum_banks[5 + b][:],
+                out=psum_banks[2 + b][:],
                 lhsT=w1_codes[0][:, 0:P].bitcast(E4M3),
                 lhsT_scale=w1_sc[0][:, 0:P],
                 rhs=w1_codes[0][:].bitcast(E4M3),
@@ -164,10 +164,11 @@ def tile_list_chirp_interference_repair_kernel(
         round_plane(3, 0, nc.vector.tensor_copy)
         round_plane(3, 1, nc.scalar.copy)
         round_w1(3)
-        for h in range(2):
-            weave(page_bf[h][:], page_pairs[h][:])
-        for h in range(2):
-            quant(page_codes[h][:], page_sc[h][:], page_bf[h][:])
+        for cols in (slice(0, 256), slice(256, 512)):
+            for h in (1, 0):
+                weave(page_bf[h][cols.start][:], page_pairs[h][:, :, cols, :])
+            for h in (1, 0):
+                quant(page_codes[h][:, cols], page_sc[h][:, cols], page_bf[h][cols.start][:])
         for a in range(2):
             nc.vector.tensor_copy(vw[a][:], tabw[a][:].bitcast(U32).indirect(idx[:]))
         quant_w1(1)
@@ -209,24 +210,29 @@ def tile_list_chirp_interference_repair_kernel(
 
         projs = {}
 
-        def project(k, bank_numbers, engine_copies):
-            a, t = divmod(k, 4)
+        for k in range(8):
             if k == 4:
                 projs[k] = after_table[:, 4, :]
             else:
                 projs[k] = kt("proj%d" % k, [P, T2], F32, tag={5: "w1_raw2", 6: "w1_raw0", 7: "w1_raw1"}.get(k))[:]
+
+        def project_part(k, h, cols, bank_number, copy):
+            a, t = divmod(k, 4)
+            bank = psum_banks[bank_number]
+            nc.tensor.matmul_mx(
+                out=bank[:, cols],
+                lhsT=w1_codes[a][:, P * t : P * t + P].bitcast(E4M3),
+                lhsT_scale=w1_sc[a][:, P * t : P * t + P],
+                rhs=page_codes[h][:, cols].bitcast(E4M3),
+                rhs_scale=page_sc[h][:, cols],
+                start=True,
+                stop=True,
+            )
+            copy(projs[k][:, 512 * h + cols.start : 512 * h + cols.stop], bank[:, cols])
+
+        def project(k, bank_numbers, engine_copies):
             for h in range(2):
-                bank = psum_banks[bank_numbers[h]]
-                nc.tensor.matmul_mx(
-                    out=bank[:],
-                    lhsT=w1_codes[a][:, P * t : P * t + P].bitcast(E4M3),
-                    lhsT_scale=w1_sc[a][:, P * t : P * t + P],
-                    rhs=page_codes[h][:].bitcast(E4M3),
-                    rhs_scale=page_sc[h][:],
-                    start=True,
-                    stop=True,
-                )
-                engine_copies[h](projs[k][:, 512 * h : 512 * h + 512], bank[:])
+                project_part(k, h, slice(0, 512), bank_numbers[h], engine_copies[h])
 
         def pick(k):
             nc.vector.tensor_copy(dirty[k // 2][:, k % 2, :], projs[k].indirect(idx3[:]))
@@ -314,9 +320,9 @@ def tile_list_chirp_interference_repair_kernel(
         halves = [slice(0, 256), slice(256, 512)]
         scalar, vector = nc.scalar.copy, nc.vector.tensor_copy
         pieces = [
-            (slice(0, 256), [(6, [0, 1], scalar), (2, [2, 3], scalar)]),
+            (slice(0, 256), [(6, [0, 1], scalar), (7, [2, 3], scalar)]),
             (slice(256, 384), [(4, [0, 1, 2, 3], scalar)]),
-            (slice(384, 512), [(3, [0, 1], scalar), (7, [2, 3], vector)]),
+            (slice(384, 512), [(3, [0, 1], scalar), (2, [2, 3], vector)]),
         ]
 
         def finish(u):
@@ -325,20 +331,21 @@ def tile_list_chirp_interference_repair_kernel(
             for cols in halves:
                 shrink(u, cols)
 
-        project(0, (0, 1), (scalar, scalar))
+        for cols in halves:
+            for h in (1, 0):
+                for k in (0, 2, 3):
+                    project_part(k, h, cols, 2 * k + h, scalar)
         project(1, (2, 3), (vector, vector))
-        project(2, (4, 5), (scalar, scalar))
-        project(3, (6, 7), (scalar, scalar))
         project(5, (0, 1), (scalar, scalar))
         project(6, (4, 5), (scalar, scalar))
-        project(7, (6, 2), (scalar, scalar))
+        project(7, (6, 7), (scalar, scalar))
         for k in range(4):
             pick(k)
-        project(4, (0, 1), (vector, vector))
+        project(4, (0, 1), (scalar, vector))
         for k in range(4, 8):
             pick(k)
-        clean_product(0, (0, 2, 1, 3), (3, 4, 7, 5))
-        clean_product(1, (0, 2), (6, 4, 2, 5))
+        clean_product(0, (0, 2, 1, 3), (3, 4, 2, 5))
+        clean_product(1, (0, 2), (6, 4, 7, 5))
         for u in range(2):
             for e in range(2):
                 magnitude(u, slice(e, e + 1), whole)
@@ -347,15 +354,15 @@ def tile_list_chirp_interference_repair_kernel(
             for e in range(2):
                 nc.gpsimd.tensor_tensor(planar[:, e, :], roots[u][:, e, :], roots[u][:, e, :], ALU.mult)
             recips[u] = planar.rearrange("p e j -> p j e")
-        clean_magnitude(0, (0, 2, 1, 3), (3, 4, 7, 5))
+        clean_magnitude(0, (0, 2, 1, 3), (3, 4, 2, 5))
         turn_clean(0, 0, 0)
         turn_clean(0, 1, 1)
         turn_clean(1, 0, 3)
-        turn_clean(1, 1, 7)
+        turn_clean(1, 1, 2)
         for u in range(2):
             finish(u)
-        clean_product(1, (1, 3), (6, 4, 2, 5))
-        clean_magnitude(1, (0, 2, 1, 3), (6, 4, 2, 5))
+        clean_product(1, (1, 3), (6, 4, 7, 5))
+        clean_magnitude(1, (0, 2, 1, 3), (6, 4, 7, 5))
         for cols in halves:
             weave_z(0, cols)
         for cols in halves:
@@ -379,7 +386,7 @@ def tile_list_chirp_interference_repair_kernel(
             limit(u, halves[0])
             shrink(u, halves[0])
         leave(*pieces[0])
-        turn_clean(3, 1, 7)
+        turn_clean(3, 1, 2)
         for cols, groups in pieces[1:]:
             for u in (2, 3):
                 magnitude(u, slice(0, 2), cols)

@@ -25,13 +25,12 @@ def tile_list_chirp_interference_repair_kernel(
     nc = tc.nc
     with ExitStack() as ctx:
         keep = ctx.enter_context(tc.tile_pool(name="keep", bufs=1))
-        ring = ctx.enter_context(tc.tile_pool(name="ring", bufs=2))
         psum = ctx.enter_context(tc.psum_pool(name="psum", bufs=1))
 
         def kt(name, shape, dtype, tag=None):
             return keep.tile(shape, dtype, name=name, tag=tag or name, align_bytes=64)
 
-        psum_banks = [psum.tile([P, 512], F32, name="bank%d" % b) for b in range(8)]
+        banks = [psum.tile([P, 512], F32, name="bank%d" % b) for b in range(8)]
         idx = keep.tile([P, S // 16], U16, name="idx")
         idx2 = keep.tile([P, S // 16], U16, name="idx2")
         idx3 = keep.tile([P, S // 16], U16, name="idx3")
@@ -99,8 +98,8 @@ def tile_list_chirp_interference_repair_kernel(
         load_w1(2)
         nc.sync.dma_start(floor[:], nf.rearrange("(a p t) -> p a t", a=2, t=4))
         load_plane(3)
-        load_w1(3)
         load_tab(0)
+        load_w1(3)
         load_tab(1)
         for q in range(4):
             move_scales(q)
@@ -109,13 +108,16 @@ def tile_list_chirp_interference_repair_kernel(
         nc.sync.dma_start(wow[:], wo_words.rearrange("a p n i -> p a (n i)").bitcast(I32))
         load_scales(nc.sync, wos, wo_scales)
 
-        page_pairs = [kt("page_pairs%d" % h, [P, 2, 512, 2], BF16) for h in range(2)]
+        page_bf = [kt("page_bf%d" % c, [P, 256, 4], BF16) for c in range(4)]
 
         def land(i):
             nc.vector.tensor_copy(page[i][:].indirect(idx2[:]), new[i][:])
 
-        def round_plane(i, h, copy):
-            copy(page_pairs[h][:, i // 2, :, i % 2], page[i][:, 512 * h : 512 * h + 512])
+        def round_lane(i, c, copy):
+            copy(page_bf[c][:, :, i], page[i][:, 256 * c : 256 * c + 256])
+
+        def gpsimd_round(dst, src):
+            nc.gpsimd.tensor_scalar(dst, src, 1.0, 0.0, ALU.mult, ALU.add)
 
         w1_bf = [kt("w1_bf%d" % a, [P, 2048], BF16) for a in range(2)]
         w1_codes = {}
@@ -140,20 +142,21 @@ def tile_list_chirp_interference_repair_kernel(
         def quant(codes, scales, woven):
             nc.vector.quantize_mx(out=codes.bitcast(E4M3), scales=scales, in_=woven.rearrange("p c t -> p (c t)"))
 
-        page_bf = [{c: kt("page_bf%d_%d" % (h, c), [P, 256, 4], BF16) for c in (0, 256)} for h in range(2)]
         page_codes = [kt("page_codes%d" % h, [P, 512], U32) for h in range(2)]
         page_sc = [kt("page_sc%d" % h, [P, 512], U8) for h in range(2)]
 
         for i in range(3):
             land(i)
-            round_plane(i, 0, nc.scalar.copy)
-            round_plane(i, 1, nc.scalar.copy)
+            round_lane(i, 2, gpsimd_round)
+            round_lane(i, 0, gpsimd_round)
+            round_lane(i, 3, nc.scalar.copy)
+            round_lane(i, 1, nc.scalar.copy)
             round_w1(i)
         land(3)
         quant_w1(0)
         for b in range(2):
             nc.tensor.matmul_mx(
-                out=psum_banks[2 + b][:],
+                out=banks[2 + b][:],
                 lhsT=w1_codes[0][:, 0:P].bitcast(E4M3),
                 lhsT_scale=w1_sc[0][:, 0:P],
                 rhs=w1_codes[0][:].bitcast(E4M3),
@@ -161,66 +164,66 @@ def tile_list_chirp_interference_repair_kernel(
                 start=True,
                 stop=True,
             )
-        round_plane(3, 0, nc.vector.tensor_copy)
-        round_plane(3, 1, nc.scalar.copy)
+        def quant_page(c):
+            h, first = c // 2, 256 * (c % 2)
+            quant(page_codes[h][:, first : first + 256], page_sc[h][:, first : first + 256], page_bf[c][:])
+
+        round_lane(3, 3, nc.scalar.copy)
         round_w1(3)
-        for cols in (slice(0, 256), slice(256, 512)):
-            for h in (1, 0):
-                weave(page_bf[h][cols.start][:], page_pairs[h][:, :, cols, :])
-            for h in (1, 0):
-                quant(page_codes[h][:, cols], page_sc[h][:, cols], page_bf[h][cols.start][:])
+        round_lane(3, 0, nc.vector.tensor_copy)
+        quant_page(3)
+        round_lane(3, 2, nc.vector.tensor_copy)
+        quant_page(0)
+        round_lane(3, 1, nc.vector.tensor_copy)
+        quant_page(2)
+        quant_page(1)
         for a in range(2):
             nc.vector.tensor_copy(vw[a][:], tabw[a][:].bitcast(U32).indirect(idx[:]))
         quant_w1(1)
 
-        clean = [[kt("clean%d%d" % (a, jt), [P, 4, P], F32) for jt in range(4)] for a in range(2)]
+        clean = [[kt("clean%d%d" % (a, jt), [P, 4, P], F32)[:] for jt in range(4)] for a in range(2)]
 
-        def clean_product(h, column_tiles, bank_numbers):
-            for jt in column_tiles:
-                bank = psum_banks[bank_numbers[jt]]
-                cols = slice(P * jt, P * jt + P)
-                for a in range(2):
-                    nc.tensor.matmul_mx(
-                        out=bank[:],
-                        lhsT=vw[a][:, cols].bitcast(E4M3),
-                        lhsT_scale=vs[:, a, cols],
-                        rhs=w2w[:, a, 1024 * h : 1024 * h + 1024].bitcast(E2M1),
-                        rhs_scale=w2s[:, a, 512 * h : 512 * h + 512],
-                        start=(a == 0),
-                        stop=(a == 1),
-                    )
+        def clean_product(a, jt, bank):
+            cols = slice(P * jt, P * jt + P)
+            for g in range(2):
+                nc.tensor.matmul_mx(
+                    out=banks[bank][:],
+                    lhsT=vw[g][:, cols].bitcast(E4M3),
+                    lhsT_scale=vs[:, g, cols],
+                    rhs=w2w[:, g, 1024 * a : 1024 * a + 1024].bitcast(E2M1),
+                    rhs_scale=w2s[:, g, 512 * a : 512 * a + 512],
+                    start=(g == 0),
+                    stop=(g == 1),
+                )
 
-        def clean_magnitude(h, column_tiles, bank_numbers):
-            for jt in column_tiles:
-                bank = psum_banks[bank_numbers[jt]]
-                nc.scalar.activation(clean[h][jt][:], bank[:].rearrange("p (m t) -> p t m", t=4), ACT.Abs)
+        def clean_magnitude(a, jt, bank):
+            nc.scalar.activation(clean[a][jt], banks[bank][:].rearrange("p (m t) -> p t m", t=4), ACT.Abs)
 
-        recip_pairs = [kt("recip%d" % a, [P, 2, 2 * S], F32) for a in range(2)]
-        recips = [recip_pairs[u // 2][:, u % 2, :].rearrange("p (j e) -> p j e", e=2) for u in range(4)]
+        def clean_bank(a, jt, bank):
+            clean_product(a, jt, bank)
+            clean_magnitude(a, jt, bank)
+
         after_table = kt("after_table", [P, 5, T2], F32, tag="picked_rows")
-        dirty_pairs = [
-            after_table[:, 2 * a : 2 * a + 2, :].rearrange("p u (e j) -> p u e j", e=2) for a in range(2)
-        ]
-        dirty = [dirty_pairs[u // 2][:, u % 2, :, :] for u in range(4)]
-        z_pairs = [kt("z_pairs%d" % a, [P, 2, S, 2], BF16) for a in range(2)]
-        root_pairs = [kt("root%d" % a, [P, 2, 2, S], F32) for a in range(2)]
-        roots = [root_pairs[u // 2][:, u % 2, :, :] for u in range(4)]
-        mag_pairs = [kt("mag%d" % a, [P, 2, 2, S], F32, tag="mag") for a in range(2)]
-        ratios, spread = {}, {}
+        dirty = [after_table[:, u, :].rearrange("p (e j) -> p e j", e=2) for u in range(4)]
+        first_projs = kt("first_projs", [P, 4, T2], F32, tag="w1_raw3")
+        projs = [first_projs[:, k, :] for k in range(4)]
+        projs.append(after_table[:, 4, :])
+        projs.append(kt("proj5", [P, T2], F32, tag="w1_raw2")[:])
+        projs.append(kt("proj6", [P, T2], F32, tag="w1_raw0")[:])
+        projs.append(kt("proj7", [P, T2], F32)[:])
+        mags = [kt("mag%d" % k, [P, S], F32, tag="new%d" % k)[:] for k in range(2)]
+        mags.extend([projs[7][:, 256:768], kt("mag3", [P, S], F32)[:]])
+        first_pairs = [kt("z_pairs0_%d" % h, [P, 2, 256, 2], BF16) for h in range(2)]
+        roots = [kt("root%d" % k, [P, S], F32)[:] for k in range(3)]
+        roots.append(first_pairs[0][:].rearrange("p u c e -> p (u c e)").bitcast(F32))
+        recips = [kt("recip%d" % u, [P, 2, S], F32, tag="page%d" % (3 * u)) for u in range(2)]
+        z_codes = [kt("z_codes%d" % a, [P, S], U32) for a in range(2)]
+        z_sc = [kt("z_sc%d" % a, [P, S], U8) for a in range(2)]
 
-        projs = {}
-
-        for k in range(8):
-            if k == 4:
-                projs[k] = after_table[:, 4, :]
-            else:
-                projs[k] = kt("proj%d" % k, [P, T2], F32, tag={5: "w1_raw2", 6: "w1_raw0", 7: "w1_raw1"}.get(k))[:]
-
-        def project_part(k, h, cols, bank_number, copy):
+        def project(k, h, bank, copy, cols=slice(0, 512)):
             a, t = divmod(k, 4)
-            bank = psum_banks[bank_number]
             nc.tensor.matmul_mx(
-                out=bank[:, cols],
+                out=banks[bank][:, cols],
                 lhsT=w1_codes[a][:, P * t : P * t + P].bitcast(E4M3),
                 lhsT_scale=w1_sc[a][:, P * t : P * t + P],
                 rhs=page_codes[h][:, cols].bitcast(E4M3),
@@ -228,79 +231,65 @@ def tile_list_chirp_interference_repair_kernel(
                 start=True,
                 stop=True,
             )
-            copy(projs[k][:, 512 * h + cols.start : 512 * h + cols.stop], bank[:, cols])
+            copy(projs[k][:, 512 * h + cols.start : 512 * h + cols.stop], banks[bank][:, cols])
 
-        def project(k, bank_numbers, engine_copies):
-            for h in range(2):
-                project_part(k, h, slice(0, 512), bank_numbers[h], engine_copies[h])
+        def plane(k):
+            return dirty[k // 2][:, k % 2, :]
 
         def pick(k):
-            nc.vector.tensor_copy(dirty[k // 2][:, k % 2, :], projs[k].indirect(idx3[:]))
+            nc.vector.tensor_copy(plane(k), projs[k].indirect(idx3[:]))
 
-        def magnitude(u, planes, cols):
-            nc.scalar.activation(mag_pairs[u // 2][:, u % 2, planes, cols], dirty[u][:, planes, cols], ACT.Abs)
+        def magnitude(k):
+            nc.scalar.activation(mags[k], plane(k), ACT.Abs)
 
-        def inverse_root(u, cols):
-            for e in range(2):
-                a, t = divmod(2 * u + e, 4)
-                nc.scalar.activation(
-                    roots[u][:, e, cols],
-                    mag_pairs[a][:, u % 2, e, cols],
-                    ACT.Abs_reciprocal_sqrt,
-                    bias=floor[:, a, t : t + 1],
-                )
+        def inverse_root(dst, src, k):
+            a, t = divmod(k, 4)
+            nc.scalar.activation(dst, src, ACT.Abs_reciprocal_sqrt, bias=floor[:, a, t : t + 1])
 
-        def inverse(pairs, cols):
-            a = pairs[0] // 2
-            us = slice(pairs[0] % 2, pairs[-1] % 2 + 1)
-            nc.scalar.activation(
-                recip_pairs[a][:, us, :].rearrange("p u (j e) -> p u j e", e=2)[:, :, cols, :],
-                root_pairs[a][:, us, :, cols].rearrange("p u e j -> p u j e"),
-                ACT.Square,
-            )
+        def inverse(k):
+            inverse_root(roots[k], mags[k], k)
+            nc.gpsimd.tensor_tensor(recips[k // 2][:, k % 2, :], roots[k], roots[k], ALU.mult)
 
-        def turn_clean(u, h, bank_number):
-            bank = psum_banks[bank_number][:].rearrange("p (e j) -> p e j", e=2)
-            for e in range(2):
-                for jj in range(2):
-                    nc.tensor.transpose(
-                        bank[:, e, P * jj : P * jj + P], clean[u // 2][2 * h + jj][:, 2 * (u % 2) + e, :], ident[:]
-                    )
-            spread[u, h] = bank.rearrange("p e j -> p j e")
+        def side_by_side(pair):
+            return pair.rearrange("p e j -> p j e")
 
-        def limit(u, cols):
-            if cols.start == 0:
-                ratios[u] = ring.tile([P, S, 2], F32, name="ratio", align_bytes=64)
-            h = cols.start // 256
-            inside = slice(cols.start - 256 * h, cols.stop - 256 * h)
-            nc.vector.tensor_tensor(ratios[u][:, cols, :], spread[u, h][:, inside, :], recips[u][:, cols, :], ALU.mult)
+        def shrink(dst, limit, values):
+            nc.vector.scalar_tensor_tensor(dst, limit, 1.0, values, ALU.min, ALU.mult)
 
-        def shrink(u, cols):
-            nc.vector.scalar_tensor_tensor(
-                z_pairs[u // 2][:, u % 2, cols, :],
-                ratios[u][:, cols, :],
-                1.0,
-                dirty[u][:, :, cols].rearrange("p e j -> p j e"),
-                ALU.min,
-                ALU.mult,
-            )
+        def turned(a, u, cols, bank_number, first):
+            width = cols.stop - cols.start
+            bank = banks[bank_number][:, first : first + 2 * width].rearrange("p (e j) -> p e j", e=2)
+            for jj, jt in enumerate(range(cols.start // P, cols.stop // P)):
+                for e in range(2):
+                    nc.tensor.transpose(bank[:, e, P * jj : P * jj + P], clean[a][jt][:, 2 * u + e, :], ident[:])
+            return side_by_side(bank)
 
-        z_codes = [kt("z_codes%d" % a, [P, S], U32) for a in range(2)]
-        z_sc = [kt("z_sc%d" % a, [P, S], U8) for a in range(2)]
+        def limits(a, cols, spread, inverses):
+            width = cols.stop - cols.start
+            limit = [kt("limit%d_%d_%d" % (a, cols.start, u), [P, width, 2], F32) for u in range(2)]
+            for u in range(2):
+                nc.vector.tensor_tensor(limit[u][:], spread[u], inverses[u], ALU.mult)
+            return limit
+
+        def product(a, u, cols, pairs, limit):
+            shrink(pairs[:, u, :, :], limit[u][:], side_by_side(dirty[2 * a + u][:, :, cols]))
+
+        def quant_z(a, cols, woven):
+            quant(z_codes[a][:, cols], z_sc[a][:, cols], woven[:])
+
+        scalar, vector = nc.scalar.copy, nc.vector.tensor_copy
         out_rows = out.rearrange("(n p) j -> p n j", p=P)
-        z_bf = {}
-
-        def weave_z(a, cols):
-            z_bf[a, cols.start] = kt("z_bf%d%d" % (a, cols.start), [P, cols.stop - cols.start, 4], BF16)
-            weave(z_bf[a, cols.start][:], z_pairs[a][:, :, cols, :])
-
-        def quant_z(a, cols):
-            quant(z_codes[a][:, cols], z_sc[a][:, cols], z_bf[a, cols.start][:])
+        halves = [slice(0, 256), slice(256, 512)]
+        pieces = [
+            (slice(0, 256), [(6, [0, 1], scalar), (7, [2, 3], scalar)]),
+            (slice(256, 384), [(2, [0, 1, 2, 3], scalar)]),
+            (slice(384, 512), [(4, [0, 1], scalar), (5, [2, 3], vector)]),
+        ]
 
         def synth(a, cols, groups):
             width = cols.stop - cols.start
             for bank, tiles, copy in groups:
-                sums = psum_banks[bank][:, 0 : width * len(tiles)].rearrange("p (i j) -> p i j", j=width)
+                sums = banks[bank][:, 0 : width * len(tiles)].rearrange("p (i j) -> p i j", j=width)
                 for i, nt in enumerate(tiles):
                     nc.tensor.matmul_mx(
                         out=sums[:, i, :],
@@ -311,90 +300,88 @@ def tile_list_chirp_interference_repair_kernel(
                         start=(a == 0 and i == 0),
                         stop=(a == 1 and i == len(tiles) - 1),
                     )
-                if a == 1:
-                    res = kt("res%d" % bank, [P, len(tiles), width], F32)
-                    copy(res[:], sums)
-                    nc.sync.dma_start(out_rows[:, tiles[0] : tiles[-1] + 1, cols], res[:])
 
-        whole = slice(0, S)
-        halves = [slice(0, 256), slice(256, 512)]
-        scalar, vector = nc.scalar.copy, nc.vector.tensor_copy
-        pieces = [
-            (slice(0, 256), [(6, [0, 1], scalar), (7, [2, 3], scalar)]),
-            (slice(256, 384), [(4, [0, 1, 2, 3], scalar)]),
-            (slice(384, 512), [(3, [0, 1], scalar), (2, [2, 3], vector)]),
-        ]
+        def store(cols, groups):
+            width = cols.stop - cols.start
+            for bank, tiles, copy in groups:
+                sums = banks[bank][:, 0 : width * len(tiles)].rearrange("p (i j) -> p i j", j=width)
+                res = kt("res%d" % bank, [P, len(tiles), width], F32)
+                copy(res[:], sums)
+                nc.sync.dma_start(out_rows[:, tiles[0] : tiles[-1] + 1, cols], res[:])
 
-        def finish(u):
-            for cols in halves:
-                limit(u, cols)
-            for cols in halves:
-                shrink(u, cols)
-
-        for cols in halves:
+        for h, cols in ((1, halves[1]), (0, halves[0]), (1, halves[0]), (0, halves[1])):
+            for k, first in ((0, 0), (1, 4), (2, 6), (3, 2)):
+                project(k, h, first + h, scalar, cols)
+        for k, first in ((5, 4), (6, 6)):
             for h in (1, 0):
-                for k in (0, 2, 3):
-                    project_part(k, h, cols, 2 * k + h, scalar)
-        project(1, (2, 3), (vector, vector))
-        project(5, (0, 1), (scalar, scalar))
-        project(6, (4, 5), (scalar, scalar))
-        project(7, (6, 7), (scalar, scalar))
-        for k in range(4):
+                project(k, h, first + h, scalar)
+        pick(0)
+        pick(1)
+        for h in (1, 0):
+            project(4, h, h, vector)
+        for k in range(2, 7):
             pick(k)
-        project(4, (0, 1), (scalar, vector))
-        for k in range(4, 8):
-            pick(k)
-        clean_product(0, (0, 2, 1, 3), (3, 4, 2, 5))
-        clean_product(1, (0, 2), (6, 4, 7, 5))
-        for u in range(2):
-            for e in range(2):
-                magnitude(u, slice(e, e + 1), whole)
-            inverse_root(u, whole)
-            planar = recip_pairs[0][:, u, :].rearrange("p (e j) -> p e j", e=2)
-            for e in range(2):
-                nc.gpsimd.tensor_tensor(planar[:, e, :], roots[u][:, e, :], roots[u][:, e, :], ALU.mult)
-            recips[u] = planar.rearrange("p e j -> p j e")
-        clean_magnitude(0, (0, 2, 1, 3), (3, 4, 2, 5))
-        turn_clean(0, 0, 0)
-        turn_clean(0, 1, 1)
-        turn_clean(1, 0, 3)
-        turn_clean(1, 1, 2)
-        for u in range(2):
-            finish(u)
-        clean_product(1, (1, 3), (6, 4, 7, 5))
-        clean_magnitude(1, (0, 2, 1, 3), (6, 4, 7, 5))
-        for cols in halves:
-            weave_z(0, cols)
-        for cols in halves:
-            quant_z(0, cols)
-        turn_clean(2, 0, 0)
-        turn_clean(3, 0, 1)
-        turn_clean(2, 1, 3)
-        for cols, groups in pieces[:2]:
+        magnitude(0)
+        magnitude(1)
+        inverse(0)
+        inverse(1)
+        magnitude(2)
+        clean_bank(0, 0, 4)
+        inverse(2)
+        magnitude(3)
+        project(7, 1, 3, scalar)
+        project(7, 0, 2, scalar)
+        inverse(3)
+        clean_bank(0, 1, 5)
+        clean_bank(0, 2, 6)
+        clean_bank(0, 3, 7)
+        pick(7)
+        first_woven = [kt("z_bf0_%d" % h, [P, 256, 4], BF16) for h in range(2)]
+        for h, cols in enumerate(halves):
+            spread = [turned(0, u, cols, 4 + 2 * h + u, 0) for u in range(2)]
+            limit = limits(0, cols, spread, [side_by_side(recips[u][:, :, cols]) for u in range(2)])
+            for u in range(2):
+                product(0, u, cols, first_pairs[h], limit)
+        for h in range(2):
+            weave(first_woven[h][:], first_pairs[h][:])
+        for h, cols in enumerate(halves):
+            quant_z(0, cols, first_woven[h])
+
+        clean_bank(1, 0, 0)
+        widths = [cols.stop - cols.start for cols, groups in pieces]
+        woven = [kt("z_bf1_%d" % n, [P, width, 4], BF16) for n, width in enumerate(widths)]
+        pairs = [kt("z_pairs1_%d" % n, [P, 2, width, 2], BF16) for n, width in enumerate(widths)]
+        for n, (cols, groups) in enumerate(pieces):
+            width = widths[n]
+            clean_bank(1, n + 1, 1 - n % 2)
+            mag = [kt("mag_%d%d" % (n, u), [P, 2, width], F32) for u in range(2)]
+            root = [kt("root_%d%d" % (n, u), [P, 2, width], F32)[:] for u in range(2 if n == 0 else 1)]
+            if n > 0:
+                words = woven[n - 1][:].rearrange("p c t -> p (c t)").bitcast(F32)
+                root.append(words[:, 0 : 2 * width].rearrange("p (e j) -> p e j", e=2))
+            recip = [kt("recip_%d%d" % (n, u), [P, width, 2], F32) for u in range(2)]
+            for u in range(2):
+                nc.scalar.activation(mag[u][:], dirty[2 + u][:, :, cols], ACT.Abs)
+            for u in range(2):
+                for e in range(2):
+                    inverse_root(root[u][:, e, :], mag[u][:, e, :], 4 + 2 * u + e)
+            for u in range(2):
+                nc.scalar.activation(recip[u][:], side_by_side(root[u]), ACT.Square)
+            if n == 0:
+                spread = [turned(1, u, cols, 2 + u, 0) for u in range(2)]
+            else:
+                spread = [turned(1, u, cols, 3 + n, 256 * u) for u in range(2)]
+            limit = limits(1, cols, spread, [recip[u][:] for u in range(2)])
             synth(0, cols, groups)
-
-        def leave(cols, groups):
-            weave_z(1, cols)
-            quant_z(1, cols)
-            synth(1, cols, groups)
-
-        for u in (2, 3):
-            magnitude(u, slice(0, 2), halves[0])
-        for u in (2, 3):
-            inverse_root(u, halves[0])
-            inverse([u], halves[0])
-            limit(u, halves[0])
-            shrink(u, halves[0])
-        leave(*pieces[0])
-        turn_clean(3, 1, 2)
-        for cols, groups in pieces[1:]:
-            for u in (2, 3):
-                magnitude(u, slice(0, 2), cols)
-            for u in (2, 3):
-                inverse_root(u, cols)
-                inverse([u], cols)
-                limit(u, cols)
-                shrink(u, cols)
-            if cols.stop == S:
-                synth(0, cols, groups)
-            leave(cols, groups)
+            if n > 0:
+                weave(woven[n - 1][:], pairs[n - 1][:])
+            product(1, 0, cols, pairs[n], limit)
+            if n > 0:
+                quant_z(1, pieces[n - 1][0], woven[n - 1])
+                synth(1, *pieces[n - 1])
+            product(1, 1, cols, pairs[n], limit)
+        weave(woven[-1][:], pairs[-1][:])
+        quant_z(1, pieces[-1][0], woven[-1])
+        synth(1, *pieces[-1])
+        for cols, groups in pieces:
+            store(cols, groups)

@@ -133,10 +133,10 @@ def tile_list_chirp_interference_repair_kernel(
             w1_sc[a] = kt("w1_sc%d" % a, [P, 512], U8, tag="page%d" % (2 - a))
             nc.vector.quantize_mx(out=w1_codes[a][:].bitcast(E4M3), scales=w1_sc[a][:], in_=w1_bf[a][:])
 
-        def weave(woven, pairs):
-            nc.vector.tensor_copy(
-                woven.rearrange("p c t -> p (c t)").bitcast(I32).rearrange("p (c u) -> p c u", u=2),
-                pairs.rearrange("p u c e -> p u (c e)").bitcast(I32).rearrange("p u c -> p c u"),
+        def weave(woven, pairs, copy=nc.vector.tensor_copy, word=I32):
+            copy(
+                woven.rearrange("p c t -> p (c t)").bitcast(word).rearrange("p (c u) -> p c u", u=2),
+                pairs.rearrange("p u c e -> p u (c e)").bitcast(word).rearrange("p u c -> p c u"),
             )
 
         def quant(codes, scales, woven):
@@ -154,16 +154,7 @@ def tile_list_chirp_interference_repair_kernel(
             round_w1(i)
         land(3)
         quant_w1(0)
-        for b in range(2):
-            nc.tensor.matmul_mx(
-                out=banks[2 + b][:],
-                lhsT=w1_codes[0][:, 0:P].bitcast(E4M3),
-                lhsT_scale=w1_sc[0][:, 0:P],
-                rhs=w1_codes[0][:].bitcast(E4M3),
-                rhs_scale=w1_sc[0][:],
-                start=True,
-                stop=True,
-            )
+
         def quant_page(c):
             h, first = c // 2, 256 * (c % 2)
             quant(page_codes[h][:, first : first + 256], page_sc[h][:, first : first + 256], page_bf[c][:])
@@ -264,11 +255,9 @@ def tile_list_chirp_interference_repair_kernel(
                     nc.tensor.transpose(bank[:, e, P * jj : P * jj + P], clean[a][jt][:, 2 * u + e, :], ident[:])
             return side_by_side(bank)
 
-        def limits(a, cols, spread, inverses):
-            width = cols.stop - cols.start
-            limit = [kt("limit%d_%d_%d" % (a, cols.start, u), [P, width, 2], F32) for u in range(2)]
-            for u in range(2):
-                nc.vector.tensor_tensor(limit[u][:], spread[u], inverses[u], ALU.mult)
+        def ratio(a, u, cols, spread, inverse):
+            limit = kt("limit%d_%d_%d" % (a, cols.start, u), [P, cols.stop - cols.start, 2], F32)
+            nc.vector.tensor_tensor(limit[:], spread, inverse, ALU.mult)
             return limit
 
         def product(a, u, cols, pairs, limit):
@@ -281,9 +270,9 @@ def tile_list_chirp_interference_repair_kernel(
         out_rows = out.rearrange("(n p) j -> p n j", p=P)
         halves = [slice(0, 256), slice(256, 512)]
         pieces = [
-            (slice(0, 256), [(6, [0, 1], scalar), (7, [2, 3], scalar)]),
-            (slice(256, 384), [(2, [0, 1, 2, 3], scalar)]),
-            (slice(384, 512), [(4, [0, 1], scalar), (5, [2, 3], vector)]),
+            (slice(0, 256), [(3, [0, 1], scalar), (1, [2, 3], scalar)]),
+            (slice(256, 384), [(4, [0, 1], scalar), (2, [2, 3], vector)]),
+            (slice(384, 512), [(6, [0, 1], scalar), (5, [2, 3], vector)]),
         ]
 
         def synth(a, cols, groups):
@@ -309,9 +298,13 @@ def tile_list_chirp_interference_repair_kernel(
                 copy(res[:], sums)
                 nc.sync.dma_start(out_rows[:, tiles[0] : tiles[-1] + 1, cols], res[:])
 
-        for h, cols in ((1, halves[1]), (0, halves[0]), (1, halves[0]), (0, halves[1])):
-            for k, first in ((0, 0), (1, 4), (2, 6), (3, 2)):
-                project(k, h, first + h, scalar, cols)
+        first_banks = (0, 4, 6, 2)
+        for h, cols in ((1, halves[1]), (0, halves[0])):
+            for k in range(4):
+                project(k, h, first_banks[k] + h, scalar, cols)
+        for k in range(4):
+            for h, cols in ((1, halves[0]), (0, halves[1])):
+                project(k, h, first_banks[k] + h, scalar, cols)
         for k, first in ((5, 4), (6, 6)):
             for h in (1, 0):
                 project(k, h, first + h, scalar)
@@ -339,13 +332,10 @@ def tile_list_chirp_interference_repair_kernel(
         first_woven = [kt("z_bf0_%d" % h, [P, 256, 4], BF16) for h in range(2)]
         for h, cols in enumerate(halves):
             spread = [turned(0, u, cols, 4 + 2 * h + u, 0) for u in range(2)]
-            limit = limits(0, cols, spread, [side_by_side(recips[u][:, :, cols]) for u in range(2)])
+            limit = [ratio(0, u, cols, spread[u], side_by_side(recips[u][:, :, cols])) for u in range(2)]
             for u in range(2):
                 product(0, u, cols, first_pairs[h], limit)
-        for h in range(2):
-            weave(first_woven[h][:], first_pairs[h][:])
-        for h, cols in enumerate(halves):
-            quant_z(0, cols, first_woven[h])
+            weave(first_woven[h][:], first_pairs[h][:], nc.gpsimd.tensor_copy)
 
         clean_bank(1, 0, 0)
         widths = [cols.stop - cols.start for cols, groups in pieces]
@@ -358,7 +348,7 @@ def tile_list_chirp_interference_repair_kernel(
             root = [kt("root_%d%d" % (n, u), [P, 2, width], F32)[:] for u in range(2 if n == 0 else 1)]
             if n > 0:
                 words = woven[n - 1][:].rearrange("p c t -> p (c t)").bitcast(F32)
-                root.append(words[:, 0 : 2 * width].rearrange("p (e j) -> p e j", e=2))
+                root.insert(0, words[:, 0 : 2 * width].rearrange("p (e j) -> p e j", e=2))
             recip = [kt("recip_%d%d" % (n, u), [P, width, 2], F32) for u in range(2)]
             for u in range(2):
                 nc.scalar.activation(mag[u][:], dirty[2 + u][:, :, cols], ACT.Abs)
@@ -371,15 +361,27 @@ def tile_list_chirp_interference_repair_kernel(
                 spread = [turned(1, u, cols, 2 + u, 0) for u in range(2)]
             else:
                 spread = [turned(1, u, cols, 3 + n, 256 * u) for u in range(2)]
-            limit = limits(1, cols, spread, [recip[u][:] for u in range(2)])
-            synth(0, cols, groups)
-            if n > 0:
-                weave(woven[n - 1][:], pairs[n - 1][:])
-            product(1, 0, cols, pairs[n], limit)
-            if n > 0:
-                quant_z(1, pieces[n - 1][0], woven[n - 1])
-                synth(1, *pieces[n - 1])
-            product(1, 1, cols, pairs[n], limit)
+            limit = [ratio(1, 0, cols, spread[0], recip[0][:])]
+            if n == 1:
+                weave(woven[0][:], pairs[0][:])
+            if n == 2:
+                weave(woven[1][:], pairs[1][:], scalar, U32)
+            limit.append(ratio(1, 1, cols, spread[1], recip[1][:]))
+            if n == 0:
+                for h in range(2):
+                    quant_z(0, halves[h], first_woven[h])
+                synth(0, cols, groups[:1])
+            if n == 1:
+                quant_z(1, pieces[0][0], woven[0])
+                synth(0, cols, groups)
+            if n == 2:
+                synth(0, pieces[0][0], pieces[0][1][1:])
+                synth(1, *pieces[0])
+                synth(0, cols, groups)
+            for u in range(2):
+                product(1, u, cols, pairs[n], limit)
+        quant_z(1, pieces[1][0], woven[1])
+        synth(1, *pieces[1])
         weave(woven[-1][:], pairs[-1][:])
         quant_z(1, pieces[-1][0], woven[-1])
         synth(1, *pieces[-1])

@@ -205,8 +205,7 @@ def tile_list_chirp_interference_repair_kernel(
         mags = [kt("mag%d" % k, [P, S], F32, tag="new%d" % k)[:] for k in range(2)]
         mags.extend([projs[7][:, 256:768], kt("mag3", [P, S], F32)[:]])
         first_pairs = [kt("z_pairs0_%d" % h, [P, 2, 256, 2], BF16) for h in range(2)]
-        roots = [kt("root%d" % k, [P, S], F32)[:] for k in range(3)]
-        roots.append(first_pairs[0][:].rearrange("p u c e -> p (u c e)").bitcast(F32))
+        roots = [kt("root%d" % k, [P, S], F32)[:] for k in range(4)]
         recips = [kt("recip%d" % u, [P, 2, S], F32, tag="page%d" % (3 * u)) for u in range(2)]
         z_codes = [kt("z_codes%d" % a, [P, S], U32) for a in range(2)]
         z_sc = [kt("z_sc%d" % a, [P, S], U8) for a in range(2)]
@@ -255,13 +254,18 @@ def tile_list_chirp_interference_repair_kernel(
                     nc.tensor.transpose(bank[:, e, P * jj : P * jj + P], clean[a][jt][:, 2 * u + e, :], ident[:])
             return side_by_side(bank)
 
+        first_res = kt("first_res", [P, 4, 256], F32)
+
         def ratio(a, u, cols, spread, inverse):
-            limit = kt("limit%d_%d_%d" % (a, cols.start, u), [P, cols.stop - cols.start, 2], F32)
-            nc.vector.tensor_tensor(limit[:], spread, inverse, ALU.mult)
+            if (a, u, cols.start) == (1, 1, 256):
+                limit = first_res[:].rearrange("p n j -> p (n j)")[:, 384:640].rearrange("p (j e) -> p j e", e=2)
+            else:
+                limit = kt("limit%d_%d_%d" % (a, cols.start, u), [P, cols.stop - cols.start, 2], F32)[:]
+            nc.vector.tensor_tensor(limit, spread, inverse, ALU.mult)
             return limit
 
         def product(a, u, cols, pairs, limit):
-            shrink(pairs[:, u, :, :], limit[u][:], side_by_side(dirty[2 * a + u][:, :, cols]))
+            shrink(pairs[:, u, :, :], limit[u], side_by_side(dirty[2 * a + u][:, :, cols]))
 
         def quant_z(a, cols, woven):
             quant(z_codes[a][:, cols], z_sc[a][:, cols], woven[:])
@@ -270,9 +274,9 @@ def tile_list_chirp_interference_repair_kernel(
         out_rows = out.rearrange("(n p) j -> p n j", p=P)
         halves = [slice(0, 256), slice(256, 512)]
         pieces = [
-            (slice(0, 256), [(3, [0, 1], scalar), (1, [2, 3], scalar)]),
-            (slice(256, 384), [(4, [0, 1], scalar), (2, [2, 3], vector)]),
-            (slice(384, 512), [(6, [0, 1], scalar), (5, [2, 3], vector)]),
+            (slice(0, 256), [(0, [0, 1], scalar), (4, [2, 3], scalar)]),
+            (slice(256, 384), [(7, [0, 1], scalar), (2, [2, 3], vector)]),
+            (slice(384, 512), [(6, [0, 1], scalar), (3, [2, 3], vector)]),
         ]
 
         def synth(a, cols, groups):
@@ -294,16 +298,14 @@ def tile_list_chirp_interference_repair_kernel(
             width = cols.stop - cols.start
             for bank, tiles, copy in groups:
                 sums = banks[bank][:, 0 : width * len(tiles)].rearrange("p (i j) -> p i j", j=width)
-                res = kt("res%d" % bank, [P, len(tiles), width], F32)
-                copy(res[:], sums)
-                nc.sync.dma_start(out_rows[:, tiles[0] : tiles[-1] + 1, cols], res[:])
+                rows = slice(tiles[0], tiles[-1] + 1)
+                res = kt("res%d" % bank, [P, len(tiles), width], F32)[:] if cols.start else first_res[:, rows]
+                copy(res, sums)
+                nc.sync.dma_start(out_rows[:, rows, cols], res)
 
         first_banks = (0, 4, 6, 2)
-        for h, cols in ((1, halves[1]), (0, halves[0])):
+        for h, cols in ((1, halves[1]), (0, halves[0]), (1, halves[0]), (0, halves[1])):
             for k in range(4):
-                project(k, h, first_banks[k] + h, scalar, cols)
-        for k in range(4):
-            for h, cols in ((1, halves[0]), (0, halves[1])):
                 project(k, h, first_banks[k] + h, scalar, cols)
         for k, first in ((5, 4), (6, 6)):
             for h in (1, 0):
@@ -326,42 +328,56 @@ def tile_list_chirp_interference_repair_kernel(
         project(7, 0, 2, scalar)
         inverse(3)
         clean_bank(0, 1, 5)
+        early_mag = kt("early_mag", [P, 2, 256], F32)
+        early_roots = [first_pairs[0][:, 0].rearrange("p c e -> p (c e)").bitcast(F32), kt("early_root", [P, 256], F32)[:]]
+        early_recip = kt("early_recip", [P, 2, 256], F32)
+        for e in range(2):
+            nc.scalar.activation(early_mag[:, e, :], dirty[2][:, e, halves[0]], ACT.Abs)
+        inverse_root(early_roots[0], early_mag[:, 0, :], 4)
+        nc.gpsimd.tensor_tensor(early_recip[:, 0, :], early_roots[0], early_roots[0], ALU.mult)
         clean_bank(0, 2, 6)
         clean_bank(0, 3, 7)
         pick(7)
         first_woven = [kt("z_bf0_%d" % h, [P, 256, 4], BF16) for h in range(2)]
         for h, cols in enumerate(halves):
-            spread = [turned(0, u, cols, 4 + 2 * h + u, 0) for u in range(2)]
+            spread = [turned(0, u, cols, 6 * h + u, 0) for u in range(2)]
             limit = [ratio(0, u, cols, spread[u], side_by_side(recips[u][:, :, cols])) for u in range(2)]
             for u in range(2):
                 product(0, u, cols, first_pairs[h], limit)
             weave(first_woven[h][:], first_pairs[h][:], nc.gpsimd.tensor_copy)
 
-        clean_bank(1, 0, 0)
+        clean_bank(1, 0, 4)
         widths = [cols.stop - cols.start for cols, groups in pieces]
         woven = [kt("z_bf1_%d" % n, [P, width, 4], BF16) for n, width in enumerate(widths)]
         pairs = [kt("z_pairs1_%d" % n, [P, 2, width, 2], BF16) for n, width in enumerate(widths)]
         for n, (cols, groups) in enumerate(pieces):
             width = widths[n]
-            clean_bank(1, n + 1, 1 - n % 2)
-            mag = [kt("mag_%d%d" % (n, u), [P, 2, width], F32) for u in range(2)]
-            root = [kt("root_%d%d" % (n, u), [P, 2, width], F32)[:] for u in range(2 if n == 0 else 1)]
+            clean_bank(1, n + 1, (3, 5, 4)[n])
+            left = range(0 if n else 1, 2)
+            mag = {u: kt("mag_%d%d" % (n, u), [P, 2, width], F32) for u in left}
+            root = {1: kt("root_%d" % n, [P, 2, width], F32)[:]}
             if n > 0:
                 words = woven[n - 1][:].rearrange("p c t -> p (c t)").bitcast(F32)
-                root.insert(0, words[:, 0 : 2 * width].rearrange("p (e j) -> p e j", e=2))
-            recip = [kt("recip_%d%d" % (n, u), [P, width, 2], F32) for u in range(2)]
-            for u in range(2):
+                root[0] = words[:, 0 : 2 * width].rearrange("p (e j) -> p e j", e=2)
+            recip = {u: kt("recip_%d%d" % (n, u), [P, width, 2], F32) for u in left}
+            for u in left:
                 nc.scalar.activation(mag[u][:], dirty[2 + u][:, :, cols], ACT.Abs)
-            for u in range(2):
+            if n == 0:
+                inverse_root(early_roots[1], early_mag[:, 1, :], 5)
+            for u in left:
                 for e in range(2):
                     inverse_root(root[u][:, e, :], mag[u][:, e, :], 4 + 2 * u + e)
-            for u in range(2):
-                nc.scalar.activation(recip[u][:], side_by_side(root[u]), ACT.Square)
             if n == 0:
-                spread = [turned(1, u, cols, 2 + u, 0) for u in range(2)]
+                nc.scalar.activation(early_recip[:, 1, :], early_roots[1], ACT.Square)
+            for u in left:
+                nc.scalar.activation(recip[u][:], side_by_side(root[u]), ACT.Square)
+            if n == 2:
+                synth(0, pieces[0][0], pieces[0][1][1:])
+            if n == 0:
+                spread = [turned(1, u, cols, 2 - 2 * u, 0) for u in range(2)]
             else:
-                spread = [turned(1, u, cols, 3 + n, 256 * u) for u in range(2)]
-            limit = [ratio(1, 0, cols, spread[0], recip[0][:])]
+                spread = [turned(1, u, cols, 2 * n - 1, 256 * u) for u in range(2)]
+            limit = [ratio(1, 0, cols, spread[0], recip[0][:] if n else side_by_side(early_recip[:]))]
             if n == 1:
                 weave(woven[0][:], pairs[0][:])
             if n == 2:
@@ -375,7 +391,6 @@ def tile_list_chirp_interference_repair_kernel(
                 quant_z(1, pieces[0][0], woven[0])
                 synth(0, cols, groups)
             if n == 2:
-                synth(0, pieces[0][0], pieces[0][1][1:])
                 synth(1, *pieces[0])
                 synth(0, cols, groups)
             for u in range(2):

@@ -87,9 +87,9 @@ def tile_list_chirp_interference_repair_kernel(
             nc.sync.dma_start(w1_raw[g][:], w1_rows[:, :, 256 * g : 256 * g + 256])
 
         nc.sync.dma_start(idx[:], offs)
-        nc.sync.dma_start(idx2[:], offs2)
         nc.vector.tensor_copy(picked_rows[:], tabs[:].indirect(idx[:]))
         load_plane(0)
+        nc.sync.dma_start(idx2[:], offs2)
         load_w1(0)
         load_plane(1)
         nc.sync.dma_start(idx3[:], offs3)
@@ -258,7 +258,7 @@ def tile_list_chirp_interference_repair_kernel(
 
         def ratio(a, u, cols, spread, inverse):
             if (a, u, cols.start) == (1, 1, 256):
-                limit = first_res[:].rearrange("p n j -> p (n j)")[:, 384:640].rearrange("p (j e) -> p j e", e=2)
+                limit = first_res[:].rearrange("p n j -> p (n j)")[:, 128:384].rearrange("p (j e) -> p j e", e=2)
             else:
                 limit = kt("limit%d_%d_%d" % (a, cols.start, u), [P, cols.stop - cols.start, 2], F32)[:]
             nc.vector.tensor_tensor(limit, spread, inverse, ALU.mult)
@@ -274,9 +274,9 @@ def tile_list_chirp_interference_repair_kernel(
         out_rows = out.rearrange("(n p) j -> p n j", p=P)
         halves = [slice(0, 256), slice(256, 512)]
         pieces = [
-            (slice(0, 256), [(0, [0, 1], scalar), (4, [2, 3], scalar)]),
+            (slice(0, 256), [(0, [0], scalar), (5, [1], scalar), (6, [2, 3], scalar)]),
             (slice(256, 384), [(7, [0, 1], scalar), (2, [2, 3], vector)]),
-            (slice(384, 512), [(6, [0, 1], scalar), (3, [2, 3], vector)]),
+            (slice(384, 512), [(1, [0, 1], scalar), (4, [2], vector), (3, [3], vector)]),
         ]
 
         def synth(a, cols, groups):
@@ -296,12 +296,13 @@ def tile_list_chirp_interference_repair_kernel(
 
         def store(cols, groups):
             width = cols.stop - cols.start
+            res = kt("res%d" % cols.start, [P, 4, width], F32) if cols.start else first_res
             for bank, tiles, copy in groups:
                 sums = banks[bank][:, 0 : width * len(tiles)].rearrange("p (i j) -> p i j", j=width)
-                rows = slice(tiles[0], tiles[-1] + 1)
-                res = kt("res%d" % bank, [P, len(tiles), width], F32)[:] if cols.start else first_res[:, rows]
-                copy(res, sums)
-                nc.sync.dma_start(out_rows[:, rows, cols], res)
+                copy(res[:, tiles[0] : tiles[-1] + 1], sums)
+                if tiles != [2]:
+                    rows = slice(min(tiles[0], 2), tiles[-1] + 1)
+                    nc.sync.dma_start(out_rows[:, rows, cols], res[:, rows])
 
         first_banks = (0, 4, 6, 2)
         for h, cols in ((1, halves[1]), (0, halves[0]), (1, halves[0]), (0, halves[1])):
@@ -349,7 +350,8 @@ def tile_list_chirp_interference_repair_kernel(
         clean_bank(1, 0, 4)
         widths = [cols.stop - cols.start for cols, groups in pieces]
         woven = [kt("z_bf1_%d" % n, [P, width, 4], BF16) for n, width in enumerate(widths)]
-        pairs = [kt("z_pairs1_%d" % n, [P, 2, width, 2], BF16) for n, width in enumerate(widths)]
+        pairs = [kt("z_pairs1_%d" % n, [P, 2, widths[n], 2], BF16)[:] for n in (0, 2)]
+        pairs.insert(1, first_res[:, 2, :].bitcast(BF16).rearrange("p (u c e) -> p u c e", u=2, e=2))
         for n, (cols, groups) in enumerate(pieces):
             width = widths[n]
             clean_bank(1, n + 1, (3, 5, 4)[n])
@@ -371,33 +373,31 @@ def tile_list_chirp_interference_repair_kernel(
                 nc.scalar.activation(early_recip[:, 1, :], early_roots[1], ACT.Square)
             for u in left:
                 nc.scalar.activation(recip[u][:], side_by_side(root[u]), ACT.Square)
-            if n == 2:
-                synth(0, pieces[0][0], pieces[0][1][1:])
             if n == 0:
                 spread = [turned(1, u, cols, 2 - 2 * u, 0) for u in range(2)]
             else:
                 spread = [turned(1, u, cols, 2 * n - 1, 256 * u) for u in range(2)]
             limit = [ratio(1, 0, cols, spread[0], recip[0][:] if n else side_by_side(early_recip[:]))]
             if n == 1:
-                weave(woven[0][:], pairs[0][:])
+                weave(woven[0][:], pairs[0])
             if n == 2:
-                weave(woven[1][:], pairs[1][:], scalar, U32)
+                weave(woven[1][:], pairs[1], scalar, U32)
             limit.append(ratio(1, 1, cols, spread[1], recip[1][:]))
             if n == 0:
                 for h in range(2):
                     quant_z(0, halves[h], first_woven[h])
-                synth(0, cols, groups[:1])
             if n == 1:
+                synth(0, *pieces[0])
                 quant_z(1, pieces[0][0], woven[0])
                 synth(0, cols, groups)
-            if n == 2:
                 synth(1, *pieces[0])
+            if n == 2:
                 synth(0, cols, groups)
             for u in range(2):
                 product(1, u, cols, pairs[n], limit)
         quant_z(1, pieces[1][0], woven[1])
         synth(1, *pieces[1])
-        weave(woven[-1][:], pairs[-1][:])
+        weave(woven[-1][:], pairs[-1])
         quant_z(1, pieces[-1][0], woven[-1])
         synth(1, *pieces[-1])
         for cols, groups in pieces:

@@ -150,7 +150,7 @@ def tile_list_chirp_interference_repair_kernel(
             round_lane(i, 2, gpsimd_round)
             round_lane(i, 0, gpsimd_round)
             round_lane(i, 3, nc.scalar.copy)
-            round_lane(i, 1, nc.scalar.copy)
+            round_lane(i, 1, gpsimd_round if i == 2 else nc.scalar.copy)
             round_w1(i)
         land(3)
         quant_w1(0)

@@ -81,31 +81,36 @@ def tile_list_chirp_interference_repair_kernel(
                 nc.sync.dma_start(vs[32 * q : 32 * q + 4, a, :].bitcast(I32), picked_rows[row : row + 4, :].bitcast(I32))
 
         def load_tab(a):
-            nc.sync.dma_start(tabw[a][:], tab_words[a].rearrange("p t i -> p (t i)").bitcast(I32))
+            words = tab_words[a].rearrange("p t i -> p (t i)").bitcast(I32)
+            for first in (0, 1024):
+                nc.sync.dma_start(tabw[a][:, first : first + 1024], words[:, first : first + 1024])
 
         def load_w1(g):
             nc.sync.dma_start(w1_raw[g][:], w1_rows[:, :, 256 * g : 256 * g + 256])
 
         nc.sync.dma_start(idx[:], offs)
         nc.vector.tensor_copy(picked_rows[:], tabs[:].indirect(idx[:]))
-        load_plane(0)
         nc.sync.dma_start(idx2[:], offs2)
+        nc.sync.dma_start(new[0][:, 0:128], xs_rows[:, 0, 0:128])
+        nc.sync.dma_start(page[0][:], base_rows[:, 0, :])
+        nc.sync.dma_start(new[0][:, 128:512], xs_rows[:, 0, 128:512])
         load_w1(0)
         load_plane(1)
-        nc.sync.dma_start(idx3[:], offs3)
         load_w1(1)
         load_plane(2)
         load_w1(2)
-        nc.sync.dma_start(floor[:], nf.rearrange("(a p t) -> p a t", a=2, t=4))
         load_plane(3)
         load_tab(0)
         load_w1(3)
         load_tab(1)
+        nc.sync.dma_start(idx3[:], offs3)
+        nc.sync.dma_start(floor[:], nf.rearrange("(a p t) -> p a t", a=2, t=4))
+        load_scales(nc.sync, w2s, w2_scales)
         for q in range(4):
             move_scales(q)
         nc.sync.dma_start(w2w[:].bitcast(I32), w2_words.rearrange("a p c -> p a c").bitcast(I32))
-        load_scales(nc.gpsimd, w2s, w2_scales)
-        nc.sync.dma_start(wow[:], wo_words.rearrange("a p n i -> p a (n i)").bitcast(I32))
+        for a in range(2):
+            nc.sync.dma_start(wow[:, a, :], wo_words[a].rearrange("p n i -> p (n i)").bitcast(I32))
         load_scales(nc.sync, wos, wo_scales)
 
         page_bf = [kt("page_bf%d" % c, [P, 256, 4], BF16) for c in range(4)]
@@ -145,8 +150,11 @@ def tile_list_chirp_interference_repair_kernel(
         page_codes = [kt("page_codes%d" % h, [P, 512], U32) for h in range(2)]
         page_sc = [kt("page_sc%d" % h, [P, 512], U8) for h in range(2)]
 
+        nc.vector.tensor_copy(page[0][:].indirect(idx2[:, 0:8]), new[0][:, 0:128])
+        nc.vector.tensor_copy(page[0][:].indirect(idx2[:, 8:32]), new[0][:, 128:512])
         for i in range(3):
-            land(i)
+            if i:
+                land(i)
             round_lane(i, 2, gpsimd_round)
             round_lane(i, 0, gpsimd_round)
             round_lane(i, 3, nc.scalar.copy)

@@ -43,20 +43,18 @@ def tile_list_chirp_interference_repair_kernel(
         vw = [kt("vw%d" % a, [P, S], U32) for a in range(2)]
         vs = kt("vs", [P, 2, S], U8)
         w2w = kt("w2w", [P, 2, 2 * H], U8)
-        w2s = kt("w2s", [P, 2, H], U8)
+        w2s = kt("w2s", [P, 2, H], U8, tag="tabs")
         wow = kt("wow", [P, 2, N], I32)
         wos = kt("wos", [P, 2, N], U8)
         floor = kt("floor", [P, 2, 4], F32)
         ident = kt("ident", [P, P], F32)
         warm = kt("warm", [P, 8], F32)
 
-        nc.scalar.dma_start(tabs[0:32, :].bitcast(I32), tab_scales.rearrange("a q t -> (a q) t").bitcast(I32))
+        nc.scalar.dma_start(tabs[96:128, :].bitcast(I32), tab_scales.rearrange("a q t -> (a q) t").bitcast(I32))
         nc.gpsimd.memset(warm[:], 1.0)
         nc.scalar.activation(warm[:, 4:5], warm[:, 0:1], ACT.Abs_reciprocal_sqrt)
-        nc.vector.memset(tabs[32:64, :].bitcast(I32), 0)
-        nc.vector.memset(tabs[64:128, :].bitcast(I32), 0)
-        nc.vector.memset(vs[:].rearrange("p a t -> p (a t)").bitcast(I32), 0)
-        nc.gpsimd.memset(w2s[:].rearrange("p a t -> p (a t)").bitcast(I32), 0)
+        nc.vector.memset(tabs[0:96, :].bitcast(I32), 0)
+        nc.gpsimd.memset(vs[:].rearrange("p a t -> p (a t)").bitcast(I32), 0)
         nc.gpsimd.memset(wos[:].rearrange("p a t -> p (a t)").bitcast(I32), 0)
         make_identity(nc, ident[:])
 
@@ -77,7 +75,7 @@ def tile_list_chirp_interference_repair_kernel(
 
         def move_scales(q):
             for a in range(2):
-                row = 16 * a + 4 * q
+                row = 96 + 16 * a + 4 * q
                 nc.sync.dma_start(vs[32 * q : 32 * q + 4, a, :].bitcast(I32), picked_rows[row : row + 4, :].bitcast(I32))
 
         def load_tab(a):
@@ -90,6 +88,7 @@ def tile_list_chirp_interference_repair_kernel(
 
         nc.sync.dma_start(idx[:], offs)
         nc.vector.tensor_copy(picked_rows[:], tabs[:].indirect(idx[:]))
+        nc.gpsimd.memset(w2s[:].rearrange("p a t -> p (a t)").bitcast(I32), 0)
         nc.sync.dma_start(idx2[:], offs2)
         nc.sync.dma_start(new[0][:, 0:128], xs_rows[:, 0, 0:128])
         nc.sync.dma_start(page[0][:], base_rows[:, 0, :])
@@ -118,8 +117,8 @@ def tile_list_chirp_interference_repair_kernel(
         def land(i):
             nc.vector.tensor_copy(page[i][:].indirect(idx2[:]), new[i][:])
 
-        def round_lane(i, c, copy):
-            copy(page_bf[c][:, :, i], page[i][:, 256 * c : 256 * c + 256])
+        def round_lane(i, c, copy, first=0, last=256):
+            copy(page_bf[c][:, first:last, i], page[i][:, 256 * c + first : 256 * c + last])
 
         def gpsimd_round(dst, src):
             nc.gpsimd.tensor_scalar(dst, src, 1.0, 0.0, ALU.mult, ALU.add)
@@ -158,7 +157,9 @@ def tile_list_chirp_interference_repair_kernel(
             round_lane(i, 2, gpsimd_round)
             round_lane(i, 0, gpsimd_round)
             round_lane(i, 3, nc.scalar.copy)
-            round_lane(i, 1, gpsimd_round if i == 2 else nc.scalar.copy)
+            if i == 2:
+                round_lane(i, 1, gpsimd_round, 0, 128)
+            round_lane(i, 1, nc.scalar.copy, 128 if i == 2 else 0)
             round_w1(i)
         land(3)
         quant_w1(0)

@@ -36,25 +36,28 @@ def tile_list_chirp_interference_repair_kernel(
         idx3 = keep.tile([P, S // 16], U16, name="idx3")
         page = [kt("page%d" % i, [P, T2], F32) for i in range(4)]
         new = [kt("new%d" % i, [P, S], F32) for i in range(4)]
-        w1_raw = [kt("w1_raw%d" % g, [P, 4, 256], F32) for g in range(4)]
+        w1_cols = (slice(0, 256), slice(256, 512), slice(512, 768), slice(768, 896), slice(896, 1024))
+        w1_raw = [kt("w1_raw%d" % g, [P, 4, cols.stop - cols.start], F32) for g, cols in enumerate(w1_cols)]
         tabw = [kt("tabw%d" % a, [P, T], I32) for a in range(2)]
         tabs = kt("tabs", [P, T], U8)
         picked_rows = kt("picked_rows", [P, S], U8)
         vw = [kt("vw%d" % a, [P, S], U32) for a in range(2)]
         vs = kt("vs", [P, 2, S], U8)
         w2w = kt("w2w", [P, 2, 2 * H], U8)
-        w2s = kt("w2s", [P, 2, H], U8, tag="tabs")
+        w2s = kt("w2s", [P, 2, H], U8)
         wow = kt("wow", [P, 2, N], I32)
         wos = kt("wos", [P, 2, N], U8)
         floor = kt("floor", [P, 2, 4], F32)
         ident = kt("ident", [P, P], F32)
         warm = kt("warm", [P, 8], F32)
 
-        nc.scalar.dma_start(tabs[96:128, :].bitcast(I32), tab_scales.rearrange("a q t -> (a q) t").bitcast(I32))
+        nc.scalar.dma_start(tabs[0:32, :].bitcast(I32), tab_scales.rearrange("a q t -> (a q) t").bitcast(I32))
         nc.gpsimd.memset(warm[:], 1.0)
         nc.scalar.activation(warm[:, 4:5], warm[:, 0:1], ACT.Abs_reciprocal_sqrt)
-        nc.vector.memset(tabs[0:96, :].bitcast(I32), 0)
-        nc.gpsimd.memset(vs[:].rearrange("p a t -> p (a t)").bitcast(I32), 0)
+        nc.vector.memset(tabs[32:64, :].bitcast(I32), 0)
+        nc.vector.memset(tabs[64:128, :].bitcast(I32), 0)
+        nc.vector.memset(vs[:].rearrange("p a t -> p (a t)").bitcast(I32), 0)
+        nc.gpsimd.memset(w2s[:].rearrange("p a t -> p (a t)").bitcast(I32), 0)
         nc.gpsimd.memset(wos[:].rearrange("p a t -> p (a t)").bitcast(I32), 0)
         make_identity(nc, ident[:])
 
@@ -75,7 +78,7 @@ def tile_list_chirp_interference_repair_kernel(
 
         def move_scales(q):
             for a in range(2):
-                row = 96 + 16 * a + 4 * q
+                row = 16 * a + 4 * q
                 nc.sync.dma_start(vs[32 * q : 32 * q + 4, a, :].bitcast(I32), picked_rows[row : row + 4, :].bitcast(I32))
 
         def load_tab(a):
@@ -84,11 +87,10 @@ def tile_list_chirp_interference_repair_kernel(
                 nc.sync.dma_start(tabw[a][:, first : first + 1024], words[:, first : first + 1024])
 
         def load_w1(g):
-            nc.sync.dma_start(w1_raw[g][:], w1_rows[:, :, 256 * g : 256 * g + 256])
+            nc.sync.dma_start(w1_raw[g][:], w1_rows[:, :, w1_cols[g]])
 
         nc.sync.dma_start(idx[:], offs)
         nc.vector.tensor_copy(picked_rows[:], tabs[:].indirect(idx[:]))
-        nc.gpsimd.memset(w2s[:].rearrange("p a t -> p (a t)").bitcast(I32), 0)
         nc.sync.dma_start(idx2[:], offs2)
         nc.sync.dma_start(new[0][:, 0:128], xs_rows[:, 0, 0:128])
         nc.sync.dma_start(page[0][:], base_rows[:, 0, :])
@@ -97,10 +99,12 @@ def tile_list_chirp_interference_repair_kernel(
         load_plane(1)
         load_w1(1)
         load_plane(2)
+        nc.sync.dma_start(new[3][:], xs_rows[:, 3, :])
         load_w1(2)
-        load_plane(3)
+        nc.sync.dma_start(page[3][:], base_rows[:, 3, :])
         load_tab(0)
         load_w1(3)
+        load_w1(4)
         load_tab(1)
         nc.sync.dma_start(idx3[:], offs3)
         nc.sync.dma_start(floor[:], nf.rearrange("(a p t) -> p a t", a=2, t=4))
@@ -108,8 +112,7 @@ def tile_list_chirp_interference_repair_kernel(
         for q in range(4):
             move_scales(q)
         nc.sync.dma_start(w2w[:].bitcast(I32), w2_words.rearrange("a p c -> p a c").bitcast(I32))
-        for a in range(2):
-            nc.sync.dma_start(wow[:, a, :], wo_words[a].rearrange("p n i -> p (n i)").bitcast(I32))
+        nc.sync.dma_start(wow[:], wo_words.rearrange("a p n i -> p a (n i)").bitcast(I32))
         load_scales(nc.sync, wos, wo_scales)
 
         page_bf = [kt("page_bf%d" % c, [P, 256, 4], BF16) for c in range(4)]
@@ -128,12 +131,13 @@ def tile_list_chirp_interference_repair_kernel(
         w1_sc = {}
 
         def round_w1(g):
-            a, half = divmod(g, 2)
+            a, first = divmod(w1_cols[g].start, 512)
+            src = w1_raw[g][:].rearrange("p j (m t) -> p m j t", t=4)
             dst = w1_bf[a][:].rearrange("p (t m j) -> p m j t", t=4, j=4)
-            nc.scalar.copy(dst[:, 64 * half : 64 * half + 64], w1_raw[g][:].rearrange("p j (m t) -> p m j t", t=4))
+            nc.scalar.copy(dst[:, first // 4 : first // 4 + src.shape[1]], src)
 
         def quant_w1(a):
-            w1_codes[a] = kt("w1_codes%d" % a, [P, 512], U32, tag="new%d" % (3 - a))
+            w1_codes[a] = kt("w1_codes%d" % a, [P, 512], U32, tag=("w1_raw2", "new2")[a])
             w1_sc[a] = kt("w1_sc%d" % a, [P, 512], U8, tag="page%d" % (2 - a))
             nc.vector.quantize_mx(out=w1_codes[a][:].bitcast(E4M3), scales=w1_sc[a][:], in_=w1_bf[a][:])
 
@@ -170,11 +174,13 @@ def tile_list_chirp_interference_repair_kernel(
 
         round_lane(3, 3, nc.scalar.copy)
         round_w1(3)
+        round_w1(4)
         round_lane(3, 0, nc.vector.tensor_copy)
+        round_lane(3, 1, nc.vector.tensor_copy, 0, 128)
         quant_page(3)
         round_lane(3, 2, nc.vector.tensor_copy)
         quant_page(0)
-        round_lane(3, 1, nc.vector.tensor_copy)
+        round_lane(3, 1, nc.vector.tensor_copy, 128)
         quant_page(2)
         quant_page(1)
         for a in range(2):
@@ -203,13 +209,13 @@ def tile_list_chirp_interference_repair_kernel(
             clean_product(a, jt, bank)
             clean_magnitude(a, jt, bank)
 
-        after_table = kt("after_table", [P, 5, T2], F32, tag="picked_rows")
+        after_table = kt("after_table", [P, 6, T2], F32, tag="picked_rows")
         dirty = [after_table[:, u, :].rearrange("p (e j) -> p e j", e=2) for u in range(4)]
         first_projs = kt("first_projs", [P, 4, T2], F32, tag="w1_raw3")
         projs = [first_projs[:, k, :] for k in range(4)]
         projs.append(after_table[:, 4, :])
-        projs.append(kt("proj5", [P, T2], F32, tag="w1_raw2")[:])
-        projs.append(kt("proj6", [P, T2], F32, tag="w1_raw0")[:])
+        projs.append(kt("proj5", [P, T2], F32, tag="w1_raw1")[:])
+        projs.append(after_table[:, 5, :])
         projs.append(kt("proj7", [P, T2], F32)[:])
         mags = [kt("mag%d" % k, [P, S], F32, tag="new%d" % k)[:] for k in range(2)]
         mags.extend([projs[7][:, 256:768], kt("mag3", [P, S], F32)[:]])
@@ -314,18 +320,24 @@ def tile_list_chirp_interference_repair_kernel(
                     nc.sync.dma_start(out_rows[:, rows, cols], res[:, rows])
 
         first_banks = (0, 4, 6, 2)
-        for h, cols in ((1, halves[1]), (0, halves[0]), (1, halves[0]), (0, halves[1])):
+        for h, cols in ((1, halves[1]), (0, halves[0])):
             for k in range(4):
                 project(k, h, first_banks[k] + h, scalar, cols)
-        for k, first in ((5, 4), (6, 6)):
-            for h in (1, 0):
-                project(k, h, first + h, scalar)
+        for k in range(4):
+            for h, cols in ((1, halves[0]), (0, halves[1])):
+                project(k, h, first_banks[k] + h, scalar, cols)
+        for h in (1, 0):
+            project(5, h, 4 + h, scalar)
+        project(6, 0, 6, scalar)
         pick(0)
         pick(1)
         for h in (1, 0):
             project(4, h, h, vector)
-        for k in range(2, 7):
-            pick(k)
+        pick(2)
+        pick(3)
+        project(6, 1, 7, lambda dst, bank: vector(dst[:, 0:256], bank[:, 0:256]))
+        pick(4)
+        pick(5)
         magnitude(0)
         magnitude(1)
         inverse(0)
@@ -334,6 +346,8 @@ def tile_list_chirp_interference_repair_kernel(
         clean_bank(0, 0, 4)
         inverse(2)
         magnitude(3)
+        scalar(projs[6][:, 768:1024], banks[7][:, 256:512])
+        pick(6)
         project(7, 1, 3, scalar)
         project(7, 0, 2, scalar)
         inverse(3)

@@ -76,15 +76,13 @@ def tile_list_chirp_interference_repair_kernel(
                     dram[:, 4 * q : 4 * q + 4, :].rearrange("a r c -> r a c").bitcast(I32),
                 )
 
-        def move_scales(q):
-            for a in range(2):
-                row = 16 * a + 4 * q
-                nc.sync.dma_start(vs[32 * q : 32 * q + 4, a, :].bitcast(I32), picked_rows[row : row + 4, :].bitcast(I32))
+        def move_scales(a, q):
+            row = 16 * a + 4 * q
+            nc.sync.dma_start(vs[32 * q : 32 * q + 4, a, :].bitcast(I32), picked_rows[row : row + 4, :].bitcast(I32))
 
-        def load_tab(a):
+        def load_tab(a, first):
             words = tab_words[a].rearrange("p t i -> p (t i)").bitcast(I32)
-            for first in (0, 1024):
-                nc.sync.dma_start(tabw[a][:, first : first + 1024], words[:, first : first + 1024])
+            nc.sync.dma_start(tabw[a][:, first : first + 1024], words[:, first : first + 1024])
 
         def load_w1(g):
             nc.sync.dma_start(w1_raw[g][:], w1_rows[:, :, w1_cols[g]])
@@ -102,15 +100,18 @@ def tile_list_chirp_interference_repair_kernel(
         nc.sync.dma_start(new[3][:], xs_rows[:, 3, :])
         load_w1(2)
         nc.sync.dma_start(page[3][:], base_rows[:, 3, :])
-        load_tab(0)
+        load_tab(0, 0)
         load_w1(3)
         load_w1(4)
-        load_tab(1)
+        move_scales(0, 0)
+        for q in range(1, 4):
+            move_scales(0, q)
+            move_scales(1, q)
+            load_tab(q // 2, 1024 * (q % 2))
         nc.sync.dma_start(idx3[:], offs3)
         nc.sync.dma_start(floor[:], nf.rearrange("(a p t) -> p a t", a=2, t=4))
         load_scales(nc.sync, w2s, w2_scales)
-        for q in range(4):
-            move_scales(q)
+        move_scales(1, 0)
         nc.sync.dma_start(w2w[:].bitcast(I32), w2_words.rearrange("a p c -> p a c").bitcast(I32))
         nc.sync.dma_start(wow[:], wo_words.rearrange("a p n i -> p a (n i)").bitcast(I32))
         load_scales(nc.sync, wos, wo_scales)
@@ -136,10 +137,15 @@ def tile_list_chirp_interference_repair_kernel(
             dst = w1_bf[a][:].rearrange("p (t m j) -> p m j t", t=4, j=4)
             nc.scalar.copy(dst[:, first // 4 : first // 4 + src.shape[1]], src)
 
-        def quant_w1(a):
-            w1_codes[a] = kt("w1_codes%d" % a, [P, 512], U32, tag=("w1_raw2", "new2")[a])
-            w1_sc[a] = kt("w1_sc%d" % a, [P, 512], U8, tag="page%d" % (2 - a))
-            nc.vector.quantize_mx(out=w1_codes[a][:].bitcast(E4M3), scales=w1_sc[a][:], in_=w1_bf[a][:])
+        def quant_w1(a, first=0, last=512):
+            if first == 0:
+                w1_codes[a] = kt("w1_codes%d" % a, [P, 512], U32, tag=("w1_raw2", "new2")[a])
+                w1_sc[a] = kt("w1_sc%d" % a, [P, 512], U8, tag="page%d" % (2 - a))
+            nc.vector.quantize_mx(
+                out=w1_codes[a][:, first:last].bitcast(E4M3),
+                scales=w1_sc[a][:, first:last],
+                in_=w1_bf[a][:, 4 * first : 4 * last],
+            )
 
         def weave(woven, pairs, copy=nc.vector.tensor_copy, word=I32):
             copy(
@@ -161,12 +167,11 @@ def tile_list_chirp_interference_repair_kernel(
             round_lane(i, 2, gpsimd_round)
             round_lane(i, 0, gpsimd_round)
             round_lane(i, 3, nc.scalar.copy)
-            if i == 2:
-                round_lane(i, 1, gpsimd_round, 0, 128)
-            round_lane(i, 1, nc.scalar.copy, 128 if i == 2 else 0)
+            round_lane(i, 1, gpsimd_round, 0, 128)
+            round_lane(i, 1, nc.scalar.copy, 128)
             round_w1(i)
         land(3)
-        quant_w1(0)
+        quant_w1(0, 0, 256)
 
         def quant_page(c):
             h, first = c // 2, 256 * (c % 2)
@@ -176,16 +181,16 @@ def tile_list_chirp_interference_repair_kernel(
         round_w1(3)
         round_w1(4)
         round_lane(3, 0, nc.vector.tensor_copy)
-        round_lane(3, 1, nc.vector.tensor_copy, 0, 128)
-        quant_page(3)
-        round_lane(3, 2, nc.vector.tensor_copy)
+        quant_w1(0, 256, 512)
         quant_page(0)
-        round_lane(3, 1, nc.vector.tensor_copy, 128)
+        round_lane(3, 2, nc.vector.tensor_copy)
+        quant_page(3)
+        round_lane(3, 1, nc.vector.tensor_copy)
         quant_page(2)
         quant_page(1)
+        quant_w1(1)
         for a in range(2):
             nc.vector.tensor_copy(vw[a][:], tabw[a][:].bitcast(U32).indirect(idx[:]))
-        quant_w1(1)
 
         clean = [[kt("clean%d%d" % (a, jt), [P, 4, P], F32)[:] for jt in range(4)] for a in range(2)]
 
@@ -209,13 +214,13 @@ def tile_list_chirp_interference_repair_kernel(
             clean_product(a, jt, bank)
             clean_magnitude(a, jt, bank)
 
-        after_table = kt("after_table", [P, 6, T2], F32, tag="picked_rows")
+        after_table = kt("after_table", [P, 5, T2], F32, tag="picked_rows")
         dirty = [after_table[:, u, :].rearrange("p (e j) -> p e j", e=2) for u in range(4)]
         first_projs = kt("first_projs", [P, 4, T2], F32, tag="w1_raw3")
         projs = [first_projs[:, k, :] for k in range(4)]
         projs.append(after_table[:, 4, :])
         projs.append(kt("proj5", [P, T2], F32, tag="w1_raw1")[:])
-        projs.append(after_table[:, 5, :])
+        projs.append(kt("proj6", [P, T2], F32, tag="w1_raw0")[:])
         projs.append(kt("proj7", [P, T2], F32)[:])
         mags = [kt("mag%d" % k, [P, S], F32, tag="new%d" % k)[:] for k in range(2)]
         mags.extend([projs[7][:, 256:768], kt("mag3", [P, S], F32)[:]])
@@ -320,24 +325,22 @@ def tile_list_chirp_interference_repair_kernel(
                     nc.sync.dma_start(out_rows[:, rows, cols], res[:, rows])
 
         first_banks = (0, 4, 6, 2)
-        for h, cols in ((1, halves[1]), (0, halves[0])):
+        for h, cols in ((0, halves[0]), (1, halves[1])):
             for k in range(4):
                 project(k, h, first_banks[k] + h, scalar, cols)
-        for k in range(4):
-            for h, cols in ((1, halves[0]), (0, halves[1])):
-                project(k, h, first_banks[k] + h, scalar, cols)
-        for h in (1, 0):
-            project(5, h, 4 + h, scalar)
-        project(6, 0, 6, scalar)
+        for first in (0, 2):
+            for h, cols in ((0, halves[1]), (1, halves[0])):
+                for k in (first, first + 1):
+                    project(k, h, first_banks[k] + h, scalar, cols)
+        for k, first in ((5, 4), (6, 6)):
+            for h in (1, 0):
+                project(k, h, first + h, scalar)
         pick(0)
         pick(1)
         for h in (1, 0):
             project(4, h, h, vector)
-        pick(2)
-        pick(3)
-        project(6, 1, 7, lambda dst, bank: vector(dst[:, 0:256], bank[:, 0:256]))
-        pick(4)
-        pick(5)
+        for k in range(2, 7):
+            pick(k)
         magnitude(0)
         magnitude(1)
         inverse(0)
@@ -346,8 +349,6 @@ def tile_list_chirp_interference_repair_kernel(
         clean_bank(0, 0, 4)
         inverse(2)
         magnitude(3)
-        scalar(projs[6][:, 768:1024], banks[7][:, 256:512])
-        pick(6)
         project(7, 1, 3, scalar)
         project(7, 0, 2, scalar)
         inverse(3)

@@ -167,8 +167,8 @@ def tile_list_chirp_interference_repair_kernel(
             round_lane(i, 2, gpsimd_round)
             round_lane(i, 0, gpsimd_round)
             round_lane(i, 3, nc.scalar.copy)
-            round_lane(i, 1, gpsimd_round, 0, 128)
-            round_lane(i, 1, nc.scalar.copy, 128)
+            round_lane(i, 1, gpsimd_round, 0, 192)
+            round_lane(i, 1, nc.scalar.copy, 192)
             round_w1(i)
         land(3)
         quant_w1(0, 0, 256)

@@ -354,12 +354,11 @@ def tile_list_chirp_interference_repair_kernel(
         inverse(3)
         clean_bank(0, 1, 5)
         early_mag = kt("early_mag", [P, 2, 256], F32)
-        early_roots = [first_pairs[0][:, 0].rearrange("p c e -> p (c e)").bitcast(F32), kt("early_root", [P, 256], F32)[:]]
+        early_roots = kt("early_root", [P, 2, 256], F32)
         early_recip = kt("early_recip", [P, 2, 256], F32)
         for e in range(2):
             nc.scalar.activation(early_mag[:, e, :], dirty[2][:, e, halves[0]], ACT.Abs)
-        inverse_root(early_roots[0], early_mag[:, 0, :], 4)
-        nc.gpsimd.tensor_tensor(early_recip[:, 0, :], early_roots[0], early_roots[0], ALU.mult)
+        inverse_root(early_roots[:, 0, :], early_mag[:, 0, :], 4)
         clean_bank(0, 2, 6)
         clean_bank(0, 3, 7)
         pick(7)
@@ -389,12 +388,12 @@ def tile_list_chirp_interference_repair_kernel(
             for u in left:
                 nc.scalar.activation(mag[u][:], dirty[2 + u][:, :, cols], ACT.Abs)
             if n == 0:
-                inverse_root(early_roots[1], early_mag[:, 1, :], 5)
+                inverse_root(early_roots[:, 1, :], early_mag[:, 1, :], 5)
             for u in left:
                 for e in range(2):
                     inverse_root(root[u][:, e, :], mag[u][:, e, :], 4 + 2 * u + e)
             if n == 0:
-                nc.scalar.activation(early_recip[:, 1, :], early_roots[1], ACT.Square)
+                nc.scalar.activation(early_recip[:], early_roots[:], ACT.Square)
             for u in left:
                 nc.scalar.activation(recip[u][:], side_by_side(root[u]), ACT.Square)
             if n == 0:

from contextlib import ExitStack

import concourse.mybir as mybir
from concourse.masks import make_identity

F32 = mybir.dt.float32
BF16 = mybir.dt.bfloat16
I32 = mybir.dt.int32
U32 = mybir.dt.uint32
U16 = mybir.dt.uint16
U8 = mybir.dt.uint8
E4M3 = mybir.dt.float8_e4m3fn_x4
E2M1 = mybir.dt.float4_e2m1fn_x4
ALU = mybir.AluOpType
ACT = mybir.ActivationFunctionType

P = 128
T, T2, S, H, N = 2048, 1024, 512, 1024, 512
FLOPS = 2684354560


def tile_list_chirp_interference_repair_kernel(
    tc, tab_words, tab_scales, offs, offs2, offs3, xs, base, w1, w2_words, w2_scales, nf, wo_words, wo_scales, out
):
    nc = tc.nc
    with ExitStack() as ctx:
        keep = ctx.enter_context(tc.tile_pool(name="keep", bufs=1))
        psum = ctx.enter_context(tc.psum_pool(name="psum", bufs=1))

        def kt(name, shape, dtype, tag=None):
            return keep.tile(shape, dtype, name=name, tag=tag or name, align_bytes=64)

        banks = [psum.tile([P, 512], F32, name="bank%d" % b) for b in range(8)]
        idx = keep.tile([P, S // 16], U16, name="idx")
        idx2 = keep.tile([P, S // 16], U16, name="idx2")
        idx3 = keep.tile([P, S // 16], U16, name="idx3")
        page = [kt("page%d" % i, [P, T2], F32) for i in range(4)]
        new = [kt("new%d" % i, [P, S], F32) for i in range(4)]
        w1_cols = (slice(0, 256), slice(256, 512), slice(512, 768), slice(768, 896), slice(896, 1024))
        w1_raw = [kt("w1_raw%d" % g, [P, 4, cols.stop - cols.start], F32) for g, cols in enumerate(w1_cols)]
        tabw = [kt("tabw%d" % a, [P, T], I32) for a in range(2)]
        tabs = kt("tabs", [P, T], U8)
        picked_rows = kt("picked_rows", [P, S], U8)
        vw = [kt("vw%d" % a, [P, S], U32) for a in range(2)]
        vs = kt("vs", [P, 2, S], U8)
        w2w = kt("w2w", [P, 2, 2 * H], U8)
        w2s = kt("w2s", [P, 2, H], U8)
        wow = kt("wow", [P, 2, N], I32)
        wos = kt("wos", [P, 2, N], U8)
        floor = kt("floor", [P, 2, 4], F32)
        ident = kt("ident", [P, P], F32)
        warm = kt("warm", [P, 8], F32)

        nc.scalar.dma_start(tabs[0:32, :].bitcast(I32), tab_scales.rearrange("a q t -> (a q) t").bitcast(I32))
        nc.gpsimd.memset(warm[:], 1.0)
        nc.scalar.activation(warm[:, 4:5], warm[:, 0:1], ACT.Abs_reciprocal_sqrt)
        nc.vector.memset(tabs[32:64, :].bitcast(I32), 0)
        nc.vector.memset(tabs[64:128, :].bitcast(I32), 0)
        nc.vector.memset(vs[:].rearrange("p a t -> p (a t)").bitcast(I32), 0)
        nc.gpsimd.memset(w2s[:].rearrange("p a t -> p (a t)").bitcast(I32), 0)
        nc.gpsimd.memset(wos[:].rearrange("p a t -> p (a t)").bitcast(I32), 0)
        make_identity(nc, ident[:])

        base_rows = base.rearrange("(p i) t -> p i t", i=4)
        xs_rows = xs.rearrange("(p i) t -> p i t", i=4)
        w1_rows = w1.rearrange("(p i) r -> p i r", i=4)

        def load_plane(i):
            nc.sync.dma_start(new[i][:], xs_rows[:, i, :])
            nc.sync.dma_start(page[i][:], base_rows[:, i, :])

        def load_scales(queue, tile, dram):
            for q in range(4):
                queue.dma_start(
                    tile[32 * q : 32 * q + 4, :, :].bitcast(I32),
                    dram[:, 4 * q : 4 * q + 4, :].rearrange("a r c -> r a c").bitcast(I32),
                )

        def move_scales(a, q):
            row = 16 * a + 4 * q
            nc.sync.dma_start(vs[32 * q : 32 * q + 4, a, :].bitcast(I32), picked_rows[row : row + 4, :].bitcast(I32))

        def load_tab(a, first):
            words = tab_words[a].rearrange("p t i -> p (t i)").bitcast(I32)
            nc.sync.dma_start(tabw[a][:, first : first + 1024], words[:, first : first + 1024])

        def load_w1(g):
            nc.sync.dma_start(w1_raw[g][:], w1_rows[:, :, w1_cols[g]])

        nc.sync.dma_start(idx[:], offs)
        nc.vector.tensor_copy(picked_rows[:], tabs[:].indirect(idx[:]))
        nc.sync.dma_start(idx2[:], offs2)
        nc.sync.dma_start(new[0][:, 0:128], xs_rows[:, 0, 0:128])
        nc.sync.dma_start(page[0][:], base_rows[:, 0, :])
        nc.sync.dma_start(new[0][:, 128:512], xs_rows[:, 0, 128:512])
        load_w1(0)
        load_plane(1)
        load_w1(1)
        load_plane(2)
        nc.sync.dma_start(new[3][:], xs_rows[:, 3, :])
        load_w1(2)
        nc.sync.dma_start(page[3][:], base_rows[:, 3, :])
        load_tab(0, 0)
        load_w1(3)
        load_w1(4)
        move_scales(0, 0)
        for q in range(1, 4):
            move_scales(0, q)
            move_scales(1, q)
            load_tab(q // 2, 1024 * (q % 2))
        nc.sync.dma_start(idx3[:], offs3)
        nc.sync.dma_start(floor[:], nf.rearrange("(a p t) -> p a t", a=2, t=4))
        load_scales(nc.sync, w2s, w2_scales)
        move_scales(1, 0)
        nc.sync.dma_start(w2w[:].bitcast(I32), w2_words.rearrange("a p c -> p a c").bitcast(I32))
        nc.sync.dma_start(wow[:], wo_words.rearrange("a p n i -> p a (n i)").bitcast(I32))
        load_scales(nc.sync, wos, wo_scales)

        page_bf = [kt("page_bf%d" % c, [P, 256, 4], BF16) for c in range(4)]

        def land(i):
            nc.vector.tensor_copy(page[i][:].indirect(idx2[:]), new[i][:])

        def round_lane(i, c, copy, first=0, last=256):
            copy(page_bf[c][:, first:last, i], page[i][:, 256 * c + first : 256 * c + last])

        def gpsimd_round(dst, src):
            nc.gpsimd.tensor_scalar(dst, src, 1.0, 0.0, ALU.mult, ALU.add)

        w1_bf = [kt("w1_bf%d" % a, [P, 2048], BF16) for a in range(2)]
        w1_codes = {}
        w1_sc = {}

        def round_w1(g):
            a, first = divmod(w1_cols[g].start, 512)
            src = w1_raw[g][:].rearrange("p j (m t) -> p m j t", t=4)
            dst = w1_bf[a][:].rearrange("p (t m j) -> p m j t", t=4, j=4)
            nc.scalar.copy(dst[:, first // 4 : first // 4 + src.shape[1]], src)

        def quant_w1(a, first=0, last=512):
            if first == 0:
                w1_codes[a] = kt("w1_codes%d" % a, [P, 512], U32, tag=("w1_raw2", "new2")[a])
                w1_sc[a] = kt("w1_sc%d" % a, [P, 512], U8, tag="page%d" % (2 - a))
            nc.vector.quantize_mx(
                out=w1_codes[a][:, first:last].bitcast(E4M3),
                scales=w1_sc[a][:, first:last],
                in_=w1_bf[a][:, 4 * first : 4 * last],
            )

        def weave(woven, pairs, copy=nc.vector.tensor_copy, word=I32):
            copy(
                woven.rearrange("p c t -> p (c t)").bitcast(word).rearrange("p (c u) -> p c u", u=2),
                pairs.rearrange("p u c e -> p u (c e)").bitcast(word).rearrange("p u c -> p c u"),
            )

        def quant(codes, scales, woven):
            nc.vector.quantize_mx(out=codes.bitcast(E4M3), scales=scales, in_=woven.rearrange("p c t -> p (c t)"))

        page_codes = [kt("page_codes%d" % h, [P, 512], U32) for h in range(2)]
        page_sc = [kt("page_sc%d" % h, [P, 512], U8) for h in range(2)]

        nc.vector.tensor_copy(page[0][:].indirect(idx2[:, 0:8]), new[0][:, 0:128])
        nc.vector.tensor_copy(page[0][:].indirect(idx2[:, 8:32]), new[0][:, 128:512])
        for i in range(3):
            if i:
                land(i)
            round_lane(i, 2, gpsimd_round)
            round_lane(i, 0, gpsimd_round)
            round_lane(i, 3, nc.scalar.copy)
            round_lane(i, 1, gpsimd_round, 0, 192)
            round_lane(i, 1, nc.scalar.copy, 192)
            round_w1(i)
        land(3)
        quant_w1(0, 0, 256)

        def quant_page(c):
            h, first = c // 2, 256 * (c % 2)
            quant(page_codes[h][:, first : first + 256], page_sc[h][:, first : first + 256], page_bf[c][:])

        round_lane(3, 3, nc.scalar.copy)
        round_w1(3)
        round_w1(4)
        round_lane(3, 0, nc.vector.tensor_copy)
        quant_w1(0, 256, 512)
        quant_page(0)
        round_lane(3, 2, nc.vector.tensor_copy)
        quant_page(3)
        round_lane(3, 1, nc.vector.tensor_copy)
        quant_page(2)
        quant_page(1)
        quant_w1(1)
        for a in range(2):
            nc.vector.tensor_copy(vw[a][:], tabw[a][:].bitcast(U32).indirect(idx[:]))

        clean = [[kt("clean%d%d" % (a, jt), [P, 4, P], F32)[:] for jt in range(4)] for a in range(2)]

        def clean_product(a, jt, bank):
            cols = slice(P * jt, P * jt + P)
            for g in range(2):
                nc.tensor.matmul_mx(
                    out=banks[bank][:],
                    lhsT=vw[g][:, cols].bitcast(E4M3),
                    lhsT_scale=vs[:, g, cols],
                    rhs=w2w[:, g, 1024 * a : 1024 * a + 1024].bitcast(E2M1),
                    rhs_scale=w2s[:, g, 512 * a : 512 * a + 512],
                    start=(g == 0),
                    stop=(g == 1),
                )

        def clean_magnitude(a, jt, bank):
            nc.scalar.activation(clean[a][jt], banks[bank][:].rearrange("p (m t) -> p t m", t=4), ACT.Abs)

        def clean_bank(a, jt, bank):
            clean_product(a, jt, bank)
            clean_magnitude(a, jt, bank)

        after_table = kt("after_table", [P, 5, T2], F32, tag="picked_rows")
        dirty = [after_table[:, u, :].rearrange("p (e j) -> p e j", e=2) for u in range(4)]
        first_projs = kt("first_projs", [P, 4, T2], F32, tag="w1_raw3")
        projs = [first_projs[:, k, :] for k in range(4)]
        projs.append(after_table[:, 4, :])
        projs.append(kt("proj5", [P, T2], F32, tag="w1_raw1")[:])
        projs.append(kt("proj6", [P, T2], F32, tag="w1_raw0")[:])
        projs.append(kt("proj7", [P, T2], F32)[:])
        mags = [kt("mag%d" % k, [P, S], F32, tag="new%d" % k)[:] for k in range(2)]
        mags.extend([projs[7][:, 256:768], kt("mag3", [P, S], F32)[:]])
        first_pairs = [kt("z_pairs0_%d" % h, [P, 2, 256, 2], BF16) for h in range(2)]
        roots = [kt("root%d" % k, [P, S], F32)[:] for k in range(4)]
        recips = [kt("recip%d" % u, [P, 2, S], F32, tag="page%d" % (3 * u)) for u in range(2)]
        z_codes = [kt("z_codes%d" % a, [P, S], U32) for a in range(2)]
        z_sc = [kt("z_sc%d" % a, [P, S], U8) for a in range(2)]

        def project(k, h, bank, copy, cols=slice(0, 512)):
            a, t = divmod(k, 4)
            nc.tensor.matmul_mx(
                out=banks[bank][:, cols],
                lhsT=w1_codes[a][:, P * t : P * t + P].bitcast(E4M3),
                lhsT_scale=w1_sc[a][:, P * t : P * t + P],
                rhs=page_codes[h][:, cols].bitcast(E4M3),
                rhs_scale=page_sc[h][:, cols],
                start=True,
                stop=True,
            )
            copy(projs[k][:, 512 * h + cols.start : 512 * h + cols.stop], banks[bank][:, cols])

        def plane(k):
            return dirty[k // 2][:, k % 2, :]

        def pick(k):
            nc.vector.tensor_copy(plane(k), projs[k].indirect(idx3[:]))

        def magnitude(k):
            nc.scalar.activation(mags[k], plane(k), ACT.Abs)

        def inverse_root(dst, src, k):
            a, t = divmod(k, 4)
            nc.scalar.activation(dst, src, ACT.Abs_reciprocal_sqrt, bias=floor[:, a, t : t + 1])

        def inverse(k):
            inverse_root(roots[k], mags[k], k)
            nc.gpsimd.tensor_tensor(recips[k // 2][:, k % 2, :], roots[k], roots[k], ALU.mult)

        def side_by_side(pair):
            return pair.rearrange("p e j -> p j e")

        def shrink(dst, limit, values):
            nc.vector.scalar_tensor_tensor(dst, limit, 1.0, values, ALU.min, ALU.mult)

        def turned(a, u, cols, bank_number, first):
            width = cols.stop - cols.start
            bank = banks[bank_number][:, first : first + 2 * width].rearrange("p (e j) -> p e j", e=2)
            for jj, jt in enumerate(range(cols.start // P, cols.stop // P)):
                for e in range(2):
                    nc.tensor.transpose(bank[:, e, P * jj : P * jj + P], clean[a][jt][:, 2 * u + e, :], ident[:])
            return side_by_side(bank)

        first_res = kt("first_res", [P, 4, 256], F32)

        def ratio(a, u, cols, spread, inverse):
            if (a, u, cols.start) == (1, 1, 256):
                limit = first_res[:].rearrange("p n j -> p (n j)")[:, 128:384].rearrange("p (j e) -> p j e", e=2)
            else:
                limit = kt("limit%d_%d_%d" % (a, cols.start, u), [P, cols.stop - cols.start, 2], F32)[:]
            nc.vector.tensor_tensor(limit, spread, inverse, ALU.mult)
            return limit

        def product(a, u, cols, pairs, limit):
            shrink(pairs[:, u, :, :], limit[u], side_by_side(dirty[2 * a + u][:, :, cols]))

        def quant_z(a, cols, woven):
            quant(z_codes[a][:, cols], z_sc[a][:, cols], woven[:])

        scalar, vector = nc.scalar.copy, nc.vector.tensor_copy
        out_rows = out.rearrange("(n p) j -> p n j", p=P)
        halves = [slice(0, 256), slice(256, 512)]
        pieces = [
            (slice(0, 256), [(0, [0], scalar), (5, [1], scalar), (6, [2, 3], scalar)]),
            (slice(256, 384), [(7, [0, 1], scalar), (2, [2, 3], vector)]),
            (slice(384, 512), [(1, [0, 1], scalar), (4, [2], vector), (3, [3], vector)]),
        ]

        def synth(a, cols, groups):
            width = cols.stop - cols.start
            for bank, tiles, copy in groups:
                sums = banks[bank][:, 0 : width * len(tiles)].rearrange("p (i j) -> p i j", j=width)
                for i, nt in enumerate(tiles):
                    nc.tensor.matmul_mx(
                        out=sums[:, i, :],
                        lhsT=wow[:, a, P * nt : P * nt + P].bitcast(E4M3),
                        lhsT_scale=wos[:, a, P * nt : P * nt + P],
                        rhs=z_codes[a][:, cols].bitcast(E4M3),
                        rhs_scale=z_sc[a][:, cols],
                        start=(a == 0 and i == 0),
                        stop=(a == 1 and i == len(tiles) - 1),
                    )

        def store(cols, groups):
            width = cols.stop - cols.start
            res = kt("res%d" % cols.start, [P, 4, width], F32) if cols.start else first_res
            for bank, tiles, copy in groups:
                sums = banks[bank][:, 0 : width * len(tiles)].rearrange("p (i j) -> p i j", j=width)
                copy(res[:, tiles[0] : tiles[-1] + 1], sums)
                if tiles != [2]:
                    rows = slice(min(tiles[0], 2), tiles[-1] + 1)
                    nc.sync.dma_start(out_rows[:, rows, cols], res[:, rows])

        first_banks = (0, 4, 6, 2)
        for h, cols in ((0, halves[0]), (1, halves[1])):
            for k in range(4):
                project(k, h, first_banks[k] + h, scalar, cols)
        for first in (0, 2):
            for h, cols in ((0, halves[1]), (1, halves[0])):
                for k in (first, first + 1):
                    project(k, h, first_banks[k] + h, scalar, cols)
        for k, first in ((5, 4), (6, 6)):
            for h in (1, 0):
                project(k, h, first + h, scalar)
        pick(0)
        pick(1)
        for h in (1, 0):
            project(4, h, h, vector)
        for k in range(2, 7):
            pick(k)
        magnitude(0)
        magnitude(1)
        inverse(0)
        inverse(1)
        magnitude(2)
        clean_bank(0, 0, 4)
        inverse(2)
        magnitude(3)
        project(7, 1, 3, scalar)
        project(7, 0, 2, scalar)
        inverse(3)
        clean_bank(0, 1, 5)
        early_mag = kt("early_mag", [P, 2, 256], F32)
        early_roots = kt("early_root", [P, 2, 256], F32)
        early_recip = kt("early_recip", [P, 2, 256], F32)
        for e in range(2):
            nc.scalar.activation(early_mag[:, e, :], dirty[2][:, e, halves[0]], ACT.Abs)
        inverse_root(early_roots[:, 0, :], early_mag[:, 0, :], 4)
        clean_bank(0, 2, 6)
        clean_bank(0, 3, 7)
        pick(7)
        first_woven = [kt("z_bf0_%d" % h, [P, 256, 4], BF16) for h in range(2)]
        for h, cols in enumerate(halves):
            spread = [turned(0, u, cols, 6 * h + u, 0) for u in range(2)]
            limit = [ratio(0, u, cols, spread[u], side_by_side(recips[u][:, :, cols])) for u in range(2)]
            for u in range(2):
                product(0, u, cols, first_pairs[h], limit)
            weave(first_woven[h][:], first_pairs[h][:], nc.gpsimd.tensor_copy)

        clean_bank(1, 0, 4)
        widths = [cols.stop - cols.start for cols, groups in pieces]
        woven = [kt("z_bf1_%d" % n, [P, width, 4], BF16) for n, width in enumerate(widths)]
        pairs = [kt("z_pairs1_%d" % n, [P, 2, widths[n], 2], BF16)[:] for n in (0, 2)]
        pairs.insert(1, first_res[:, 2, :].bitcast(BF16).rearrange("p (u c e) -> p u c e", u=2, e=2))
        for n, (cols, groups) in enumerate(pieces):
            width = widths[n]
            clean_bank(1, n + 1, (3, 5, 4)[n])
            left = range(0 if n else 1, 2)
            mag = {u: kt("mag_%d%d" % (n, u), [P, 2, width], F32) for u in left}
            root = {1: kt("root_%d" % n, [P, 2, width], F32)[:]}
            if n > 0:
                words = woven[n - 1][:].rearrange("p c t -> p (c t)").bitcast(F32)
                root[0] = words[:, 0 : 2 * width].rearrange("p (e j) -> p e j", e=2)
            recip = {u: kt("recip_%d%d" % (n, u), [P, width, 2], F32) for u in left}
            for u in left:
                nc.scalar.activation(mag[u][:], dirty[2 + u][:, :, cols], ACT.Abs)
            if n == 0:
                inverse_root(early_roots[:, 1, :], early_mag[:, 1, :], 5)
            for u in left:
                for e in range(2):
                    inverse_root(root[u][:, e, :], mag[u][:, e, :], 4 + 2 * u + e)
            if n == 0:
                nc.scalar.activation(early_recip[:], early_roots[:], ACT.Square)
            for u in left:
                nc.scalar.activation(recip[u][:], side_by_side(root[u]), ACT.Square)
            if n == 0:
                spread = [turned(1, u, cols, 2 - 2 * u, 0) for u in range(2)]
            else:
                spread = [turned(1, u, cols, 2 * n - 1, 256 * u) for u in range(2)]
            limit = [ratio(1, 0, cols, spread[0], recip[0][:] if n else side_by_side(early_recip[:]))]
            if n == 1:
                weave(woven[0][:], pairs[0])
            if n == 2:
                weave(woven[1][:], pairs[1], scalar, U32)
            limit.append(ratio(1, 1, cols, spread[1], recip[1][:]))
            if n == 0:
                for h in range(2):
                    quant_z(0, halves[h], first_woven[h])
            if n == 1:
                synth(0, *pieces[0])
                quant_z(1, pieces[0][0], woven[0])
                synth(0, cols, groups)
                synth(1, *pieces[0])
            if n == 2:
                synth(0, cols, groups)
            for u in range(2):
                product(1, u, cols, pairs[n], limit)
        quant_z(1, pieces[1][0], woven[1])
        synth(1, *pieces[1])
        weave(woven[-1][:], pairs[-1])
        quant_z(1, pieces[-1][0], woven[-1])
        synth(1, *pieces[-1])
        for cols, groups in pieces:
            store(cols, groups)
